import numpy as np, ml_dtypes
CORES = [13,21,141,149]
N = 4
BF = ml_dtypes.bfloat16
def gentries(a):
    return np.ascontiguousarray(a.reshape(8, 16, -1).transpose(0, 2, 1)).reshape(8, -1)
def gtable(e):
    e = np.asarray(e); return np.ascontiguousarray(e.reshape(8, -1, 16).transpose(0, 2, 1)).reshape(128, -1).astype(np.int32)
P, C, CAP, TH, DAYS, BITS = 1280, 3, 448, 1440, 4, 11
W = N * P; M = 2 ** BITS; B0 = TH // 16; DEC = 8; STEP = 77
def parts(rng):
    x = (rng.random((N, 8, 16, P)) * B0 * rng.random((N, 8, 1, P))).astype(np.int64); x = np.minimum(x, B0 - 1)
    return x, rng.integers(0, W, (N, 8, C * P)), rng.integers(0, M, (N, 8, C * P)), rng.integers(0, 256, (N, 8, P))
def even(rng):
    u = rng.integers(-B0, B0 + 1, (N, 8, 8, P)); u[:, :, 0] = np.abs(u[:, :, 0])
    return np.concatenate([B0 + u, B0 - u], axis=2)
def sick(rng):
    e = even(rng)
    return np.minimum(e + ((256 - e) * rng.random((N, 8, 1, P)) * rng.random(e.shape)).astype(np.int64), 255)
def lean(rng):
    n = rng.integers(-(-TH // 255), 9, (N, 8, 1, P)); s = rng.integers(0, 16, (N, 8, 1, P)); lo = -(-TH // n)
    on = (np.arange(16)[:, None] - s) % 16 < n
    return np.where(on, np.minimum(lo + ((256 - lo) * rng.random((N, 8, 16, P))).astype(np.int64), 255), 0)
def mark(rng, x, share):
    return np.where(rng.random((N, 8, 1, P)) < share, sick(rng), x)
def pack(x, nb, dice, res):
    return {"x0": np.ascontiguousarray(x.reshape(N, 128, P)).astype(np.int32), "nb": np.stack([gtable(v) for v in nb]), "dice": np.stack([gtable(v) for v in dice]), "res": np.ascontiguousarray(res).astype(np.int32)}
def setup_inputs(rng):
    x, nb, dice, res = parts(rng); share = rng.choice(np.array([0.04, 0.1, 0.2, 0.45]), (N, 8, 1, 1))
    return pack(mark(rng, x, share), nb, dice, res)
def setup_inputs_room(rng):
    x, nb, dice, res = parts(rng); m = np.zeros((N, 8, P), bool)
    n = rng.choice(np.array([0, 1, CAP - 1, CAP, CAP + 1, P]), (N, 8))
    n[0] = (CAP, CAP + 1, P, CAP - 1, 1, 0, CAP, CAP + 1)
    n[1] = (0, P, CAP + 1, 1, CAP - 1, CAP, CAP, CAP)
    n[2] = (CAP, CAP + 1, CAP, P, CAP, CAP + 1, CAP, CAP)
    n[3, ::2] = CAP
    j = P - CAP; cnt = W - int(np.sum(np.minimum(n[:, 6], CAP)))
    while -(-j * M // cnt) * cnt >= (j + 1) * M: j += 1; cnt += 1
    n[0, 6] = P - j; d = -(-j * M // cnt)
    for q in range(N):
        for g in range(8):
            o = rng.permutation(P)
            if (q == 0 and g >= 6) or (q == 1 and g == 7): o = np.arange(P)[::-1]
            if (q == 1 and g == 6) or (q == 2 and g == 7): o = np.arange(P)
            if q == 3: o = np.argsort(rng.permutation(16)[np.arange(P) % 16], kind="stable")
            m[q, g, o[:int(n[q, g])]] = True
    x = np.where(m[:, :, None, :], sick(rng), x)
    x[:, 6] = np.where(m[:, 6][:, None, :], even(rng)[:, 6], x[:, 6]); res[:, 6] = 255
    dice[:, 6] = np.where(rng.random((N, C * P)) < 0.1, d, dice[:, 6])
    return pack(x, nb, dice, res)
def setup_inputs_ties(rng):
    x, nb, dice, res = parts(rng)
    x = np.where(rng.random((N, 8, 1, P)) < 0.2, rng.choice(np.array([0, 7, 8, 9]), x.shape), x)
    x = mark(rng, x, 0.06); e = even(rng); e[:, :, 0] += rng.integers(-1, 2, (N, 8, P))
    x = np.where(rng.random((N, 8, 1, P)) < 0.35, e, x)
    x = np.where(rng.random((N, 8, 1, P)) < 0.08, lean(rng), x)
    res = np.where(rng.random(res.shape) < 0.7, rng.choice(np.array([0, 1, 7, 8, 9, 255]), res.shape), res)
    return pack(x, nb, dice, res)
def setup_inputs_ends(rng):
    x, nb, dice, res = parts(rng); x = mark(rng, x, 0.15); s = sick(rng)
    x[..., 0] = s[..., 0]; x[..., P - 1] = s[..., P - 1]
    nb[:, 1::2] = np.tile(nb[:, 1::2, :P], (1, 1, C))
    nb[:, 2] = rng.choice(np.array([0, P - 1, W - P, W - 1]), (N, C * P))
    nb[:, 4] = P * np.arange(N)[:, None] + rng.integers(0, P, (N, C * P))
    me = P * np.arange(N)[:, None] + np.tile(np.arange(P), C)[None, :]
    nb[:, 6] = np.where(rng.random((N, C * P)) < 0.5, me, nb[:, 6])
    dice = np.where(rng.random(dice.shape) < 0.8, rng.choice(np.array([0, 1, M - 1, M - 2, M - STEP, M - STEP - 1, M - 2 * STEP, M // 2]), dice.shape), dice)
    return pack(x, nb, dice, res)
def setup_inputs_cold(rng):
    x, nb, dice, res = parts(rng); share = rng.choice(np.array([0.05, 0.15, 0.3]), (N, 8, 1, 1))
    q = rng.permutation(N); c = rng.permutation(8)
    share[q[0]] = 1.0; share[q[1]] = 0.0; share[:, c[0]] = 0.0; share[:, c[1]] = 1.0; share[:, c[[2, 4, 5]]] = 0.0
    x = mark(rng, x, share); e = even(rng)
    a, v = int(rng.integers(0, N)), int(rng.integers(0, P)); x[a, c[2], :, v] = 255
    late = rng.random((N, 1, P)) < 0.25; last = np.arange(C)[:, None] == C - 1
    nb[:, c[2]] = np.where((last | ~late).reshape(N, C * P), a * P + v, nb[:, c[2]])
    nb[q[1], c[3]] = q[0] * P + rng.integers(0, CAP, C * P)
    h = rng.random((N, 1, P)) < 0.2; stay = rng.random((N, 1, P)) < 0.5; stay[q[2]] = False
    x[:, c[4]] = np.where(h, np.where(stay, 255, e[:, c[4]]), x[:, c[4]]); res[:, c[4]] = 255
    h = rng.random((N, P)) < 0.1; u = np.arange(W).reshape(N, P)
    x[:, c[5]] = np.where(h[:, None, :], rng.integers(min(B0 + DEC * DAYS, 255), 256, (N, 16, P)), x[:, c[5]]); res[:, c[5]] = rng.integers(0, 32, (N, P))
    nb[:, c[5]] = np.where(np.tile(h, (1, C)), rng.choice(u[h], (N, C * P)), rng.choice(u[~h], (N, C * P)))
    return pack(x, nb, dice, res)
def setup_inputs_spread(rng):
    x, nb, dice, res = parts(rng)
    x = np.minimum((np.exp2(8 * rng.random((N, 8, 1, P))) * rng.random((N, 8, 16, P))).astype(np.int64), 255)
    res = np.minimum(np.exp2(8 * rng.random((N, 8, P))).astype(np.int64) - 1, 255)
    nb = np.minimum((W * rng.random((N, 8, C * P)) ** rng.choice(np.array([1, 2, 3]), (N, 8, 1))).astype(np.int64), W - 1)
    dice = np.minimum((M * rng.random((N, 8, C * P)) ** 2).astype(np.int64), M - 1)
    return pack(x, nb, dice, res)
def check_inputs(d):
    bad = []
    for k, hi in (("x0", 255), ("nb", W - 1), ("dice", M - 1), ("res", 255)):
        if np.min(d[k]) < 0 or np.max(d[k]) > hi: bad.append("range of " + k)
    return bad
def reference(x0, nb, dice, res):
    x = x0.astype(np.int64).reshape(N, 8, 16, P); r = res.astype(np.int64).reshape(N, 8, 1, P)
    link = np.stack([gentries(v) for v in nb]).astype(np.int64); dr = np.stack([gentries(v) for v in dice]).astype(np.int64)
    for t in range(DAYS):
        high = (np.add.reduce(x, axis=2) >= TH).astype(np.int64); before = np.add.accumulate(high, axis=2) - high
        ill = (high == 1) & (before < CAP)
        flag = np.ascontiguousarray(ill.transpose(1, 0, 2)).reshape(8, W)
        win = np.ascontiguousarray(np.where(ill[:, :, None, :], x, 0).transpose(1, 2, 0, 3)).reshape(8, 16, W)
        come = []
        for q in range(N):
            come.append(np.maximum.reduce(np.take_along_axis(win, link[q][:, None, :], 2).reshape(8, 16, C, P), axis=2))
        d = (dr + STEP * t) & (M - 1); new = link.copy()
        for g in range(8):
            sl = np.flatnonzero(~flag[g])
            hit = flag[g][link[:, g]] & ~np.tile(ill[:, g], (1, C))
            new[:, g] = np.where(hit, sl[(d[:, g] * len(sl)) >> BITS], link[:, g])
        x = np.maximum(np.maximum(x - DEC, np.stack(come) - r), 0); link = new
    return {"yx": x.reshape(N, 128, P).astype(np.float32), "ynb": np.stack([gtable(v) for v in link]).astype(np.float32)}

@@ -1,0 +1,627 @@
+import numpy as np
+from concourse.bass import DstId, RemoteDMATransfer
+from concourse.mybir import AluOpType, ActivationFunctionType
+
+ALU = AluOpType
+ACTF = ActivationFunctionType
+N, P, C, CAP, TH, DAYS, BITS, DEC, STEP = 4, 1280, 3, 448, 1440, 4, 11, 8, 77
+W = N * P
+M = 1 << BITS
+PB = P // N
+LC = P // 16
+NL = C * LC
+Z0 = (N - 1) * P
+VOFF = 160
+LOFF = 16 * VOFF + 7.5
+
+BF, F32, I32, U16 = "bfloat16", "float32", "int32", "uint16"
+SCRATCH = {"AO": ("dram", [N, 128, 160], I32), "AL": ("dram", [N, 128, 160], I32),
+           "LD": ("dram", [N, 128, NL // N], F32), "LL": ("dram", [N, 128, NL // N], F32)}
+for _d, _l in ((I32, {"XI": P, "LI": NL, "DI": NL, "RI": LC, "ji": NL, "da": NL, "pi": 8, "pb": 8}),
+               (U16, {"so16": 32, "j16": NL, "o16": NL}),
+               (F32, {"YF": P, "hs": LC, "U": 24, "so": 24, "L": NL, "Lp": NL, "Lf": NL, "mm": NL, "tt": NL, "ww": NL,
+                      "pf": 8, "cols": 32, "r16": 144, "zf": LC, "NI": 128, "NK": 24}),
+               (BF, {"XO": P, "XL": P, "XE": P, "XS": P, "R2": 2 * LC, "S": 4 * P, "G": 4 * P, "D0": 4 * P, "WN0": 7 * P,
+                     "WN1": 7 * P, "TT": 7 * P, "DT": P + 16, "H": C * P, "SW": Z0 + 16 + W + PB, "hb": 96,
+                     "u2": 2 * LC, "u1": LC, "vals": PB, "nl": 16, "rows": 384, "ones": 896, "MB": 896, "ME": 528,
+                     "M2": 256, "LS": 144, "NW": 144, "NA": 144, "PN": 1024, "BO": 128, "SC": 128, "tmp": 768,
+                     "base": 512, "QM": 2048, "MX": 640, "crow": PB})):
+    for _k, _n in _l.items():
+        SCRATCH[_k] = ("sbuf", [128, _n], _d)
+for _b in range(8):
+    SCRATCH["ps%d" % _b] = ("psum", [128, 512], F32)
+
+SEMAPHORES = (["pe", "dve", "act", "pool", "sent", "aux"] + ["sx%d" % i for i in range(N)] + ["ex%d" % i for i in range(N)]
+              + ["el%d" % i for i in range(N)] + ["dm%d" % i for i in range(48)])
+
+CFG = {"cyc": 0.001, "pe": 0.0005, "fix": 0.06, "lat": 0.07, "gat": 1.55, "sca": 3.8, "dma": 2.0, "dbw": 250e3,
+       "hop": (3.0, 5.0), "tch": 6, "rep": 3, "parts": ((0, 640), (640, 1280)), "chunks": ((0, 640), (640, 1280)),
+       "ka": ((0, 1, 2), (0, 1, 2), (0, 1, 2), (0, 1)), "seed": 1, "bias": -0.5, "iters": 2500, "jit": 0.5, "temp": 0.15}
+STATS = {}
+
+
+def relays(T, topo, src, dst):
+    if topo.may_write(src, dst):
+        return None
+    can = [c for c in topo.cores_of(src) if c != src and T.rank_of(c) is None and topo.may_write(c, dst)]
+    same = topo.host(src) == topo.host(dst)
+    pick = [c for c in can if (topo.die(c) == topo.die(src)) == same]
+    return (pick or can)[0]
+
+
+def emask(es):
+    m = 0
+    for e in es:
+        m |= 1 << e
+    return m
+
+
+def relay_program(g, core, T, topo, s, d):
+    dst = T.cores[d]
+    rid, pid = topo.addr(dst, core)
+    es = topo.engines(core, dst)
+    xs = slice(PB * s, PB * s + PB)
+    for sem, cnt, ap in ((T.sem.aux, 4, T.AL[s]), (T.sem["sx%d" % s], 8, T.XL[:, xs]),
+                         (T.sem["ex%d" % s], 8, T.XE[:, xs]), (T.sem["el%d" % s], 4, T.LL[s])):
+        g.wait_ge(sem, cnt)
+        g.remote_dma(ap, ap, sem, T.sem.sent, pid, rid, emask(es))
+    g.wait_ge(T.sem.sent, 4 * len(es))
+
+
+def rank_program(g, core, T, topo):
+    me = T.rank_of(core)
+    if me is None:
+        for s in range(N):
+            for d in range(N):
+                if s != d and relays(T, topo, T.cores[s], T.cores[d]) == core:
+                    relay_program(g, core, T, topo, s, d)
+        return
+    cf = CFG
+    Q = {"pe": g.tensor, "dve": g.vector, "act": g.scalar, "pool": g, "sp": g.sync}
+    ops = []
+    hist = {}
+    mcache = {}
+
+    def A(name, lo=0, hi=None, step=1):
+        hi = SCRATCH[name][1][-1] if hi is None else hi
+        key = (lo, hi, step)
+        if key not in mcache:
+            mcache[key] = ((1 << (hi - lo)) - 1) << lo if step == 1 else emask(range(lo, hi, step))
+        ap = T[name][:, lo:hi] if step == 1 else T[name][:, lo:hi:step]
+        return {"ap": ap, "buf": name, "mask": mcache[key], "n": len(range(lo, hi, step)), "dt": SCRATCH[name][2]}
+
+    def slot(name, mask):
+        return {"buf": name, "mask": mask}
+
+    def add(var, rd, wr, sem=None, after=(), name=""):
+        i = len(ops)
+        pre = {}
+        for o, w in [(o, False) for o in rd] + [(o, True) for o in wr]:
+            ps = o["buf"].startswith("ps")
+            mk = 1 if ps else o["mask"]
+            lst = hist.setdefault(o["buf"], [])
+            for (j, m2, w2) in lst:
+                if j != i and m2 & mk and (ps or w or w2):
+                    pre[j] = pre.get(j, False) or not ps
+            if w or ps:
+                lst[:] = [e for e in lst if e[1] & ~mk or e[0] == i]
+            lst.append((i, mk, w))
+        for j in after:
+            pre[j] = True
+        ops.append({"var": var, "pre": pre, "sem": sem, "name": name})
+        return i
+
+    def cyc(n, k=1.0):
+        t = cf["fix"] + max(n * k, 64) * cf["cyc"]
+        return t, t
+
+    def narrow(*os_):
+        return 0.5 if all(o["dt"] in (BF, U16) for o in os_) else 1.0
+
+    def sc(x):
+        return x["ap"] if isinstance(x, dict) else x
+
+    def scs(*xs):
+        return [x for x in xs if isinstance(x, dict)]
+
+    def ts(out, in0, s1, s2, op0, op1=None, act=None, name=""):
+        def f(q):
+            if op1 is None:
+                return q.tensor_scalar(out["ap"], in0["ap"], sc(s1), None, op0)
+            return q.tensor_scalar(out["ap"], in0["ap"], sc(s1), sc(s2), op0, op1)
+        var = {"dve": cyc(out["n"], narrow(out, in0)) + (f,)}
+        if act is not None:
+            var["act"] = cyc(out["n"]) + (lambda q: q.activation(out["ap"], in0["ap"], act[0], bias=sc(act[1]), scale=sc(act[2])),)
+        return add(var, [in0] + scs(s1, s2), [out], name=name)
+
+    def scale(out, in_, s):
+        return ts(out, in_, s, None, ALU.mult, act=(ACTF.Identity, 0.0, s))
+
+    def cp(out, in0, both=True, name=""):
+        var = {"dve": cyc(out["n"], narrow(out, in0)) + (lambda q: q.tensor_copy(out["ap"], in0["ap"]),)}
+        if both:
+            var["act"] = cyc(out["n"]) + (lambda q: q.activation(out["ap"], in0["ap"], ACTF.Copy),)
+        return add(var, [in0], [out], name=name)
+
+    def tt(out, a, b, op, name=""):
+        k = 1.0 if (a["buf"].startswith("ps") or b["buf"].startswith("ps")) else 2.0
+        return add({"dve": cyc(out["n"], k) + (lambda q: q.tensor_tensor(out["ap"], a["ap"], b["ap"], op),)}, [a, b], [out], name=name)
+
+    def ms(out, v):
+        return add({"dve": cyc(out["n"], narrow(out)) + (lambda q: q.memset(out["ap"], v),)}, [], [out])
+
+    def scan(out, d0, d1, init, op0, op1, name=""):
+        return add({"dve": cyc(out["n"], narrow(out, d0, d1)) + (
+            lambda q: q.tensor_tensor_scan(out["ap"], d0["ap"], d1["ap"], sc(init), op0, op1),)}, [d0, d1] + scs(init), [out], name=name)
+
+    def mm(items, name="", start=True, stop=True):
+        t = sum(max(64, o["n"]) * (4 if r["dt"] == F32 else 1) for o, l, r in items) * cf["pe"]
+
+        def f(q):
+            ins = None
+            for i, (o, l, r) in enumerate(items):
+                ins = q.matmul(o["ap"], l["ap"], r["ap"], start and i == 0, stop and i == len(items) - 1)
+            return ins
+        return add({"pe": (t, t + 0.05, f)}, [x for o, l, r in items for x in (l, r)], [items[0][0]], name=name)
+
+    def iota(out, pattern, base, cm):
+        t = 0.13 + 2 * out["n"] * cf["cyc"]
+        if out["dt"] == I32:
+            return add({"pool": (t, t, lambda q: q.iota(out["ap"], pattern, base, cm))}, [], [out])
+        return add({"pool": (t, t, lambda q: q.iota(out["ap"], pattern, base, cm, allow_small_or_imprecise_dtypes=True))}, [], [out])
+
+    def asel(out, in_, pattern, base, cm):
+        t = 0.17 + 2 * out["n"] * cf["cyc"]
+        return add({"pool": (t, t, lambda q: q.affine_select(out["ap"], in_["ap"], pattern, ALU.is_equal, 0.0, base, cm))}, [in_], [out])
+
+    ndma = [0]
+
+    def dmas(jobs, rd, wr, nbytes, qs=("sp", "act"), after=(), name="", hold=0.1):
+        sem = T.sem["dm%d" % ndma[0]]
+        ndma[0] += 1
+
+        def f(q):
+            for o, i in jobs:
+                q.dma_start(o, i).then_inc(sem, 16)
+        return add({e: (hold, cf["dma"] + nbytes / cf["dbw"], f) for e in qs}, rd, wr, sem=(sem, 16 * len(jobs)), after=after, name=name)
+
+    def arrive(sem, cnt, wr, after, lag):
+        return add({"ext": (0.0, lag, None)}, [], wr, sem=(sem, cnt), after=after)
+
+    others = [d for d in range(N) if d != me]
+    via = {d: relays(T, topo, core, T.cores[d]) for d in others}
+    hop = {d: (via[d] if via[d] is not None else T.cores[d]) for d in others}
+    far = sorted([d for d in others if via[d] is not None], key=lambda d: topo.die(via[d]) == topo.die(core))
+    near = [d for d in others if via[d] is None]
+    sent = [0]
+
+    def xfer(d, es, src, dst, sem):
+        rid, pid = topo.addr(hop[d], core)
+        sent[0] += len(es)
+        return RemoteDMATransfer(dst_ids=[DstId(rid=rid, pnc=pid)], dma_engine_mask=emask(es), remote_sem=sem, src=src, dst=dst)
+
+    def send(trs, rd, after=()):
+        return add({"pool": (0.5, 0.5, lambda q: q.remote_dma_fused(trs, local_sem=T.sem.sent))}, rd, [], sem="none", after=after, name="send")
+
+    def send_x(src, land, sem, after=()):
+        e, d, to = topo.engines(core, hop[far[0]]), near[0], T[land][:, PB * me:PB * me + PB]
+        a = send([xfer(f, e[i::2], T[src][:, PB * f:PB * f + PB], to, sem) for i, f in enumerate(far)],
+                 [A(src, PB * f, PB * f + PB) for f in far], after)
+        b = send([xfer(d, topo.engines(core, hop[d]), T[src][:, PB * d:PB * d + PB], to, sem)], [A(src, PB * d, PB * d + PB)], [a])
+        return a, b
+
+    def send_d(src, land, sem):
+        d = near[0]
+        e0 = topo.engines(core, hop[d])
+        e = [x for x in topo.engines(core, hop[far[0]]) if x not in e0]
+        trs = [xfer(f, e[i::2], T[src][f], T[land][me], sem) for i, f in enumerate(far)]
+        return send(trs + [xfer(d, e0, T[src][d], T[land][me], sem)], [slot(src, 15)])
+
+    def got(s):
+        r = relays(T, topo, T.cores[s], core)
+        return len(topo.engines(r if r is not None else T.cores[s], core))
+
+    for d in far + near + [me]:
+        blk = A("XI", PB * d, PB * d + PB)
+        dmas([(blk["ap"], T.x0[32 * d:32 * d + 32, :])], [], [blk], 128 * PB * 4, name="ldx")
+        cp(A("XL" if d == me else "XO", PB * d, PB * d + PB), blk, both=False, name="cvx")
+    dmas([(T.AO[:, 0:48, :], T.nb[:])], [], [slot("AO", 1)], 122880)
+    dmas([(T.AO[:, 48:96, :], T.dice[:])], [], [slot("AO", 2)], 122880)
+    dmas([(T.AO[:, 96:112, :], T.res[:]), (T.AO[:, 112:128, :], T.res[:])], [], [slot("AO", 4)], 81920, hold=0.2)
+    sl = send_d("AO", "AL", T.sem.aux)
+    sa, sb = send_x("XO", "XL", T.sem["sx%d" % me], [sl])
+    dmas([(T.AL[me], T.AO[me])], [slot("AO", 7)], [slot("AL", 1)], 81920)
+    for s in near + far:
+        arrive(T.sem["sx%d" % s], got(s), [A("XL", PB * s, PB * s + PB)], [sb if s in near else sa], cf["hop"][0 if s in near else 1])
+    arrive(T.sem.aux, sum(got(s) for s in others), [slot("AL", 2)], [sl], cf["hop"][1])
+    dmas([(T.LI[:], T.AL[:, 0:48, :])], [slot("AL", 3)], [A("LI")], 122880)
+    dmas([(T.DI[:], T.AL[:, 48:96, :])], [slot("AL", 3)], [A("DI")], 122880)
+    dmas([(T.RI[:], T.AL[:, 96:112, :])], [slot("AL", 3)], [A("RI")], 40960)
+
+    def mat(name, i):
+        return A(name, 128 * i, 128 * i + 128)
+
+    def col(name, i):
+        return A(name, i, i + 1)
+
+    ms(A("ones"), 1.0)
+    ms(A("zf"), 0.0)
+    ms(A("hb"), 0.0)
+    iota(col("pi", 0), [[0, 1]], 0, 1)
+    asel(A("MB"), A("ones"), [[1, 4], [4, 224]], -384, -1)
+    asel(A("M2", 0, 128), A("ones", 0, 128), [[1, 128]], 0, -1)
+    iota(mat("rows", 0), [[0, 8], [1, 16]], 0, 0)
+    iota(mat("rows", 1), [[1, 8], [0, 16]], 0, 0)
+    iota(mat("rows", 2), [[0, 4], [1, 2], [0, 16]], 0, 0)
+    iota(A("r16"), [[1, 144]], 0, 0)
+    iota(A("crow"), [[1, PB]], -VOFF, 0)
+    asel(A("ME"), A("ones", 0, 528), [[1, 528]], -3, -4)
+    p = col("pi", 0)
+    ts(col("pb", 0), p, 15, None, ALU.bitwise_and)
+    ts(col("pb", 1), p, 4, None, ALU.logical_shift_right)
+    ts(col("pb", 2), p, 4, 1, ALU.logical_shift_right, ALU.bitwise_and)
+    ts(col("pb", 3), p, 5, None, ALU.logical_shift_right)
+    ts(col("pb", 4), p, 7, None, ALU.bitwise_and)
+    cp(A("pf", 0, 5), A("pb", 0, 5), both=False)
+    p16, pg, pc, pq, p8 = [col("pf", i) for i in range(5)]
+    ts(A("cols", 0, 8), A("r16", 0, 8), p8, -256.0, ALU.is_equal, ALU.mult)
+    ts(A("cols", 8, 12), A("r16", 0, 4), pq, None, ALU.is_equal)
+    ts(col("cols", 12), p16, 8.0, None, ALU.is_lt)
+    ts(col("cols", 13), p16, 8.0, None, ALU.is_ge)
+    ts(col("cols", 14), p16, 15.0, None, ALU.is_equal)
+    e15, thr = col("cols", 14), col("cols", 19)
+    for i, src, a, b in ((15, e15, -255.0, -1.0), (16, e15, 255.0, 1.0),
+                         (17, e15, 16.5, -0.5), (24, e15, 32768.5, -0.5),
+                         (25, e15, 1.0 / 2048 - 16, 16.0),
+                         (18, e15, -1.0 / 128, 1.0 / 128), (26, e15, 1.0, -1.0),
+                         (19, pq, P, -LOFF), (20, pg, 16.0, 15.0), (21, p16, -1.0, -W),
+                         (22, pq, -P, Z0 + 16), (23, pq, -P, Z0 + W // 2)):
+        ts(col("cols", i), src, float(a), float(b), ALU.mult, ALU.add)
+    ts(A("crow"), A("crow"), e15, col("cols", 26), ALU.mult, ALU.add)
+    IDN = mat("M2", 0)
+    if cf["rep"] < N - 1:
+        cp(mat("M2", 1), IDN)
+    ts(A("LS"), A("r16"), col("cols", 20), None, ALU.is_equal)
+    scale(A("NW"), A("LS"), col("cols", 17))
+    scale(A("NA"), A("LS"), col("cols", 24))
+    ts(A("BO"), mat("rows", 1), pg, None, ALU.is_equal)
+    ts(A("SC"), mat("rows", 2), pc, None, ALU.is_equal)
+    for r in range(8):
+        scale(mat("PN", r), A("BO"), col("cols", r))
+    ts(mat("tmp", 0), mat("rows", 0), p16, None, ALU.is_gt)
+    ts(mat("tmp", 1), mat("rows", 0), p16, None, ALU.is_le)
+    ts(mat("tmp", 2), mat("rows", 0), p16, None, ALU.is_ge)
+    ts(mat("tmp", 3), mat("rows", 0), p16, -8192.0, ALU.is_equal, ALU.mult)
+    ts(mat("tmp", 4), mat("rows", 0), 15.0, 2.0, ALU.is_lt, ALU.mult)
+    I1024, I4096, ZERO, HA, HU = [mat("MX", i) for i in range(5)]
+    scale(I1024, IDN, 1024.0)
+    scale(I4096, IDN, 4096.0)
+    scale(ZERO, IDN, 0.0)
+    scale(A("NI"), IDN, -1.0)
+    tt(mat("tmp", 5), mat("tmp", 0), A("BO"), ALU.mult)
+    tt(HA, mat("tmp", 5), I1024, ALU.subtract)
+    tt(HU, mat("tmp", 1), A("BO"), ALU.mult)
+    tt(mat("tmp", 2), mat("tmp", 2), mat("tmp", 4), ALU.mult)
+    for b in range(4):
+        tt(mat("base", b), mat("tmp", b), A("SC"), ALU.mult)
+    for q in range(N):
+        scale(A("QM", 512 * q, 512 * q + 512), A("base"), col("cols", 8 + q))
+    ts(A("NK", 0, 20), A("r16", 0, 20), -16.0, col("cols", 21), ALU.mult, ALU.add)
+    zone, fill = A("SW", Z0, Z0 + P + 16), A("SW", Z0, Z0 + P)
+    ms(zone, -256.0)
+    flat = cf["rep"] == N - 1
+    own0 = Z0 if flat else 0
+    for name in ["WN0"] * flat + ["TT"]:
+        jobs, wr = [], []
+        for s in range(1, N):
+            cut = 128 - 32 * s
+            for p0, p1, a in ((cut, 128, Z0 + P * s), (0, cut, Z0 + P * (s - N))):
+                jobs.append((T[name][p0:p1, a:a + P], T.SW[p0:p1, Z0:Z0 + P]))
+                wr.append(A(name, a, a + P))
+        dmas(jobs, [fill], wr, 983040, qs=("sp",), after=[sl, sb], hold=983040 / cf["dbw"])
+    for s in range(7 * flat):
+        if s != N - 1:
+            iota(A("WN1", P * s, P * s + P), [[0, P]], 0, 0)
+    scale(A("DT"), zone, col("cols", 18))
+    scale(A("D0", 0, 4 * P, 4), fill, 4.0)
+    for k in (1, 2):
+        scale(A("D0", k, 4 * P, 4), fill, 0.0)
+
+    def spread(name, c0, c1, first, wide):
+        jobs, wr, o = [], [], (Z0 if wide else 0)
+        for s in range(first, N):
+            cut = 128 - 32 * s
+            a, b = (o + P * s, o + P * (s - N)) if wide else (P * s, P * s)
+            jobs += [(T[name][0:cut, a + c0:a + c1], T[name][32 * s:128, o + c0:o + c1]),
+                     (T[name][cut:128, b + c0:b + c1], T[name][0:32 * s, o + c0:o + c1])]
+            wr += [A(name, a + c0, a + c1), A(name, b + c0, b + c1)]
+        nb_ = (N - first) * 256 * (c1 - c0)
+        dmas(jobs, [A(name, o + c0, o + c1)], wr, nb_, qs=("sp",), name="rep" + name, hold=nb_ / cf["dbw"])
+
+    def LSr(name, r):
+        return A(name, 15 - r, 143 - r)
+
+    def X(lo, hi, step=1):
+        return A("S", 4 * lo + 3, 4 * hi, 4 * step)
+
+    def ps(b, lo, hi, step=1):
+        return A("ps%d" % b, lo, hi, step)
+
+    for i, q in enumerate([me] + near + far):
+        for b in range(4):
+            mm([(ps(b, 0, PB), A("MB", 224 * b + 96 - 32 * q, 224 * b + 224 - 32 * q), A("XL", PB * q, PB * q + PB))], "place", i == 0, i == N - 1)
+    for b in range(4):
+        cp(X(PB * b, PB * b + PB), ps(b, 0, PB), name="x0")
+    for e in range(2):
+        ts(A("R2", LC * e, LC * e + LC), A("RI"), col("cols", 12 + e), None, ALU.mult)
+    for j, (b0, b1) in enumerate(((0, 6), (6, 12), (12, 16))):
+        for b in range(b0, b1):
+            mm([(ps(5 + j, LC * (b - b0), LC * (b - b0 + 1)), mat("PN", b % 8), A("R2", LC * (b // 8), LC * (b // 8 + 1)))])
+        scale(A("D0", 4 * LC * b0 + 3, 4 * LC * b1, 4), ps(5 + j, 0, LC * (b1 - b0)), 1.0 / 256)
+    ts(A("L"), A("LI"), -LOFF, None, ALU.add)
+
+    def offsets():
+        if flat:
+            return ts(A("o16"), A("L"), thr, float(own0), ALU.subtract, ALU.add, name="o16")
+        ts(A("ww"), A("L"), col("cols", 27), float(W), ALU.is_lt, ALU.mult, name="w")
+        tt(A("ww"), A("ww"), A("L"), ALU.add, name="o")
+        return ts(A("o16"), A("ww"), thr, None, ALU.subtract, name="o16")
+
+    if not flat:
+        ts(col("cols", 27), thr, -0.5, None, ALU.add)
+    offsets()
+    bank = [0]
+
+    def nextbank():
+        bank[0] += 1
+        return (bank[0] - 1) % 4
+
+    for t in range(DAYS):
+        wn = "WN%d" % (t % 2)
+        for p0, p1 in cf["parts"]:
+            c0, c1 = p0 // 16, p1 // 16
+            mm([(ps(4, c0, c1), LSr("LS", r), X(p0 + r, p1, 16)) for r in range(16)], "tot")
+            ts(A("hb", c0 + 1, c1 + 1), ps(4, c0, c1), float(TH), None, ALU.is_ge, name="h")
+            o = ps(4, 96 + c0, 96 + c1)
+            mm([(o, HA, A("hb", c0 + 1, c1 + 1)), (o, HU, A("hb", c0, c1)), (o, I1024, A("hb", c0, c1))], "H")
+            scan(A("hs", c0, c1), o, A("zf", c0, c1), col("hs", c0 - 1) if c0 else 0.0, ALU.add, ALU.add, name="Hs")
+            for e in range(2):
+                ts(A("u2", 2 * c0 + e, 2 * c1, 2), A("hs", c0, c1), float(CAP - 1024), col("cols", 12 + e), ALU.is_ge, ALU.mult, name="u2")
+            k = -(-(p1 - p0) // 512)
+            n = (p1 - p0) // k
+            own = [(nextbank(), p0 + n * i) for i in range(k)]
+            for b, lo in own:
+                mm([(ps(b, 0, n), IDN, X(lo, lo + n))], "Ix", True, False)
+            for b, lo in own:
+                mm([(ps(b, r, n, 8), mat("PN", r), A("u2", lo // 8, (lo + n) // 8)) for r in range(8)], "pen", False, True)
+                cp(A(wn, own0 + lo, own0 + lo + n), ps(b, 0, n), name="xm")
+            if cf["rep"]:
+                spread(wn, p0, p1, N - cf["rep"], flat)
+            for _, lo in own:
+                for s in range(1, N - cf["rep"]):
+                    b = nextbank()
+                    mm([(ps(b, 0, n), A("M2", 32 * s, 32 * s + 128), A(wn, lo, lo + n))], "perm")
+                    cp(A(wn, P * s + lo, P * s + lo + n), ps(b, 0, n), name="win")
+        ts(A("u1"), A("hs"), float(CAP - 1024), None, ALU.is_ge, name="u1")
+        for p0, p1 in cf["chunks"]:
+            ts(A("G", 4 * p0 + 3, 4 * p1, 4), X(p0, p1), float(-DEC), 0.0, ALU.add, ALU.max,
+               act=(ACTF.Relu, float(-DEC), 1.0), name="xd")
+        mm([(ps(5, 0, 5), LSr("LS", r), A("u1", r, LC, 16)) for r in range(16)], "n")
+        nl = A("nl", 0, 5)
+        cp(nl, ps(5, 0, 5), name="nl")
+        mm([(ps(5, 32, 53), ZERO, A("ones", 0, 21))]
+           + [(ps(5, 32 + 5 * q, 37 + 5 * q), mat("QM", 4 * q), nl) for q in range(N)]
+           + [(ps(5, 33 + 5 * q, 38 + 5 * q), mat("QM", 4 * q + 1), nl) for q in range(N)], "D2")
+        mm([(ps(5, 64, 84), A("NI"), A("NK", 0, 20))]
+           + [(ps(5, 64 + 5 * q, 69 + 5 * q), mat("QM", 4 * q + 3), nl) for q in range(N)], "Z")
+        scan(A("U", 0, 21), ps(5, 32, 53), A("zf", 0, 21), 0.0, ALU.add, ALU.add, name="U")
+        tt(A("so", 0, 20), A("U", 0, 20), ps(5, 64, 84), ALU.max, name="so")
+        sw, so16, vals = A("SW"), A("so16", 0, 20), A("vals")
+        ts(so16, A("so", 0, 20), col("cols", 22), None, ALU.add, name="so16")
+        mm([(ps(4, 192, 192 + PB), IDN, A("crow"))]
+           + [(ps(4, 192 + LC * q, 192 + LC * (q + 1)), mat("QM", 4 * q + 2), A("u1")) for q in range(N)], "vals")
+        cp(vals, ps(4, 192, 192 + PB), name="vals")
+        add({"dve": cyc(PB, cf["sca"]) + (lambda q: q.tensor_copy(sw["ap"].indirect(so16["ap"]), vals["ap"]),)},
+            [so16, vals], [sw], name="scat")
+        scan(A("TT", Z0 - 16, Z0 + P), A("DT"), zone, -256.0, ALU.add, ALU.max, name="Ts")
+        spread("TT", 0, P, 1, True)
+        if t < DAYS - 1:
+            iota(zone, [[0, P + 16]], -256, 0)
+        if t > 0:
+            ts(A("da"), A("DI"), float(STEP), None, ALU.add, name="da")
+            ts(A("DI"), A("da"), M - 1, None, ALU.bitwise_and, name="db")
+        scale(col("U", 21), col("U", 20), 1.0 / M)
+        ts(A("ji"), A("DI"), col("U", 21), -(W / 2 + 0.5 - 0.5 / M), ALU.mult, ALU.add, name="ji")
+        ts(A("j16"), A("ji"), col("cols", 23), None, ALU.add, name="j16")
+        win = A(wn, 0, 7 * P if flat else W)
+        for p0, p1 in cf["chunks"]:
+            n = p1 - p0
+            for k in range(C):
+                o = A("G", 4 * p0 + k, 4 * p1, 4)
+                off = A("o16", LC * k + p0 // 16, LC * k + p1 // 16)
+                add({"dve": cyc(n, cf["gat"]) + (lambda q, o=o, off=off, win=win: q.tensor_copy(o["ap"], win["ap"].indirect(off["ap"])),),
+                     "act": cyc(n, cf["gat"]) + (lambda q, o=o, off=off, win=win: q.activation(o["ap"], win["ap"].indirect(off["ap"]), ACTF.Copy),)},
+                    [win, off], [o], name="gat")
+            scan(A("S", 4 * p0, 4 * p1), A("D0", 4 * p0, 4 * p1), A("G", 4 * p0, 4 * p1), 0.0, ALU.add, ALU.max, name="xs")
+        tab, lo_, hi_, tsc = A("TT"), col("cols", 15), col("cols", 16), col("cols", 25)
+        n = C * P // cf["tch"]
+        for h in range(cf["tch"]):
+            o, off = A("H", n * h, n * h + n), A("j16", n // 16 * h, n // 16 * (h + 1))
+            if h * C // cf["tch"] in cf["ka"][t]:
+                add({"act": cyc(n, cf["gat"]) + (lambda q, o=o, off=off: q.activation(
+                    o["ap"], tab["ap"].indirect(off["ap"]), ACTF.Tanh, scale=tsc["ap"]),)}, [tab, off, tsc], [o], name="tga")
+            else:
+                add({"dve": cyc(n, cf["gat"]) + (lambda q, o=o, off=off: q.tensor_scalar(
+                    o["ap"], tab["ap"].indirect(off["ap"]), lo_["ap"], hi_["ap"], ALU.max, ALU.min),)}, [tab, off, lo_, hi_], [o], name="tg")
+        mm([(ps(7, 0, NL), A("NI"), A("L"))], "negL", True, False)
+        for k in range(C):
+            mm([(ps(7, LC * k, LC * k + LC), LSr("NA" if k in cf["ka"][t] else "NW", r), A("H", P * k + r, P * k + P, 16))
+                for r in range(16)], "N", False, k == C - 1)
+        for k in range(C):
+            o = ps(6, LC * k, LC * k + LC)
+            mm([(o, I4096, A("u1"))] + [(o, LSr("LS", r), A("G", 4 * r + k, 4 * P, 64)) for r in range(16)], "F")
+        ts(A("mm"), ps(6, 0, NL), 5000.0, None, ALU.is_gt, name="m")
+        tt(A("tt"), ps(7, 0, NL), A("mm"), ALU.mult, name="t")
+        if t == DAYS - 1:
+            ts(A("Lp"), A("L"), LOFF, None, ALU.add, act=(ACTF.Identity, LOFF, 1.0))
+            tt(A("Lp"), A("Lp"), A("tt"), ALU.add, name="Lf")
+            ts(A("Lf"), A("Lp"), 12582912.0, -12582912.0, ALU.add, ALU.add, name="round")
+        else:
+            tt(A("L"), A("L"), A("tt"), ALU.add, name="L")
+            offsets()
+
+    for d in far + near + [me]:
+        b = nextbank()
+        for j in range(4):
+            mm([(ps(b, 0, PB), A("ME", 128 * d - j + 3, 128 * d - j + 131), X(PB * j, PB * j + PB))], "back", j == 0, j == 3)
+        cp(A("YF" if d == me else "XS", PB * d, PB * d + PB), ps(b, 0, PB), name="out")
+    sa, sb = send_x("XS", "XE", T.sem["ex%d" % me])
+    dmas([(T.LD[:], T.Lf[:])], [A("Lf")], [slot("LD", 15)], 122880)
+    sl = send_d("LD", "LL", T.sem["el%d" % me])
+    dmas([(T.ynb[32 * me:32 * me + 32, :], T.Lf[32 * me:32 * me + 32, :])], [A("Lf")], [], 30720)
+    blk = A("YF", PB * me, PB * me + PB)
+    dmas([(T.yx[32 * me:32 * me + 32, :], blk["ap"])], [blk], [], 163840)
+    for s in near + far:
+        lag = cf["hop"][0 if s in near else 1]
+        land, blk = A("XE", PB * s, PB * s + PB), A("YF", PB * s, PB * s + PB)
+        arrive(T.sem["ex%d" % s], got(s), [land], [sb if s in near else sa], lag)
+        cp(blk, land, name="cvy")
+        dmas([(T.yx[32 * s:32 * s + 32, :], blk["ap"])], [blk], [], 163840)
+        arrive(T.sem["el%d" % s], got(s), [slot("LL", 1 << s)], [sl, sb], lag)
+        dmas([(T.ynb[32 * s:32 * s + 32, :], T.LL[s])], [slot("LL", 1 << s)], [], 30720)
+
+    n = len(ops)
+    succ = [[] for _ in ops]
+    for i, o in enumerate(ops):
+        for j in o["pre"]:
+            succ[j].append(i)
+    lat = cf["lat"]
+
+    def place(line, lo, busy):
+        for k, (a, b) in enumerate(line):
+            if lo + busy <= a + 1e-9:
+                return lo, k
+            lo = max(lo, b)
+        return lo, len(line)
+
+    def forward(key, bias):
+        start, eng = [0.0] * n, [None] * n
+        lines = {e: [] for e in Q}
+        left = [len(o["pre"]) for o in ops]
+        ready = [i for i in range(n) if left[i] == 0]
+        while ready:
+            i = min(ready, key=lambda x: key[x])
+            ready.remove(i)
+            best = None
+            for e, v in ops[i]["var"].items():
+                lo, k = 0.0, 0
+                for j, w in ops[i]["pre"].items():
+                    u = ops[j]["var"][eng[j]]
+                    lo = max(lo, start[j] + (u[1] + lat if (eng[j] != e or w or ops[j]["sem"] is not None) else u[0]))
+                if e != "ext":
+                    lo, k = place(lines[e], lo, v[0])
+                f = lo + v[1] + (bias[i] if e == "dve" else 0.0)
+                if best is None or f < best[0]:
+                    best = (f, lo, e, k)
+            _, start[i], eng[i], k = best
+            if eng[i] != "ext":
+                lines[eng[i]].insert(k, (start[i], start[i] + ops[i]["var"][eng[i]][0]))
+            for j in succ[i]:
+                left[j] -= 1
+                if left[j] == 0:
+                    ready.append(j)
+        return max(start[i] + ops[i]["var"][eng[i]][1] for i in range(n)), start, eng
+
+    def backward(start, eng):
+        r = [0.0] * n
+        lines = {e: [] for e in Q}
+        left = [len(x) for x in succ]
+        ready = [i for i in range(n) if left[i] == 0]
+        while ready:
+            j = max(ready, key=lambda x: start[x] + ops[x]["var"][eng[x]][1])
+            ready.remove(j)
+            u = ops[j]["var"][eng[j]]
+            lo = u[1] - u[0]
+            for i in succ[j]:
+                c = u[1] + lat if (eng[j] != eng[i] or ops[i]["pre"][j] or ops[j]["sem"] is not None) else u[0]
+                lo = max(lo, r[i] + ops[i]["var"][eng[i]][0] + c - u[0])
+            if eng[j] != "ext":
+                lo, k = place(lines[eng[j]], lo, u[0])
+                lines[eng[j]].insert(k, (lo, lo + u[0]))
+            r[j] = lo
+            for i in ops[j]["pre"]:
+                left[i] -= 1
+                if left[i] == 0:
+                    ready.append(i)
+        return [-(r[i] + ops[i]["var"][eng[i]][0]) for i in range(n)]
+
+    if "plan" not in STATS:
+        rng = np.random.default_rng(cf["seed"])
+        prio = [0.0] * n
+        for i in range(n - 1, -1, -1):
+            prio[i] = min(v[1] for v in ops[i]["var"].values()) + lat + max([prio[j] for j in succ[i]] + [0.0])
+        key, bias = [-x for x in prio], [cf["bias"]] * n
+        best = cur = None
+        for it in range(cf["iters"]):
+            span, start, eng = forward(key, bias)
+            if best is None or span <= best[0]:
+                best = (span, key, bias)
+            if cur is None or span <= cur[0] + cf["temp"] * (1 - it / cf["iters"]) * float(rng.random()):
+                cur = (span, key, bias, backward(start, eng))
+            a = float(rng.random()) * span
+            key = [x + (cf["jit"] * float(y) if a - 8 < x + span < a + 8 else 0.0) for x, y in zip(cur[3], rng.random(n))]
+            bias = [b if y > 0.03 else 4 * float(z) - 2 for b, y, z in zip(cur[2], rng.random(n), rng.random(n))]
+        STATS["plan"] = best
+    span, start, eng = forward(STATS["plan"][1], STATS["plan"][2])
+    seq = sorted(range(n), key=lambda i: (start[i], i))
+    STATS[me] = (span, [(start[i], start[i] + ops[i]["var"][eng[i]][1], eng[i], ops[i]["name"]) for i in seq])
+
+    def needs(i):
+        return [j for j, w in ops[i]["pre"].items() if ops[j]["sem"] != "none" and (eng[j] != eng[i] or w or ops[j]["sem"] is not None)]
+
+    pos = {}
+    seen = {e: {} for e in Q}
+    wanted = set()
+    for i in seq:
+        pos[i] = len(pos)
+        if eng[i] == "ext":
+            continue
+        lastof = {}
+        for j in needs(i):
+            if ops[j]["sem"] is None and pos[j] > lastof.get(eng[j], (-1, -1))[0]:
+                lastof[eng[j]] = (pos[j], j)
+        for e, (pj, j) in lastof.items():
+            if pj > seen[eng[i]].get(e, -1):
+                seen[eng[i]][e] = pj
+                wanted.add(j)
+    count = {e: 0 for e in Q}
+    val = {}
+    seen = {e: {} for e in Q}
+    waited = set()
+    for i in seq:
+        e = eng[i]
+        if e == "ext":
+            continue
+        q = Q[e]
+        top = {}
+        for j in needs(i):
+            if ops[j]["sem"] is not None:
+                if seen[e].get(j) is None:
+                    seen[e][j] = 1
+                    waited.add(j)
+                    q.wait_ge(ops[j]["sem"][0], ops[j]["sem"][1])
+            elif j in val:
+                top[eng[j]] = max(top.get(eng[j], 0), val[j])
+        for f, v in top.items():
+            if v > seen[e].get(f, 0):
+                seen[e][f] = v
+                q.wait_ge(T.sem[f], v)
+        ins = ops[i]["var"][e][2](q)
+        if i in wanted:
+            count[e] += 1
+            val[i] = count[e]
+            ins.then_inc(T.sem[e], 1)
+    for i in seq:
+        if ops[i]["sem"] not in (None, "none") and i not in waited:
+            g.wait_ge(ops[i]["sem"][0], ops[i]["sem"][1])
+    g.wait_ge(T.sem.sent, sent[0])

@@ -12,31 +12,47 @@ LC = P // 16
 NL = C * LC
 Z0 = (N - 1) * P
 VOFF = 160
-LOFF = 16 * VOFF + 7.5
+ROUND = 12582912.0
 
 BF, F32, I32, U16 = "bfloat16", "float32", "int32", "uint16"
-SCRATCH = {"AO": ("dram", [N, 128, 160], I32), "AL": ("dram", [N, 128, 160], I32),
-           "LD": ("dram", [N, 128, NL // N], F32), "LL": ("dram", [N, 128, NL // N], F32)}
-for _d, _l in ((I32, {"XI": P, "LI": NL, "DI": NL, "RI": LC, "ji": NL, "da": NL, "pi": 8, "pb": 8}),
-               (U16, {"so16": 32, "j16": NL, "o16": NL}),
-               (F32, {"YF": P, "hs": LC, "U": 24, "so": 24, "L": NL, "Lp": NL, "Lf": NL, "mm": NL, "tt": NL, "ww": NL,
-                      "pf": 8, "cols": 32, "r16": 144, "zf": LC, "NI": 128, "NK": 24}),
-               (BF, {"XO": P, "XL": P, "XE": P, "XS": P, "R2": 2 * LC, "S": 4 * P, "G": 4 * P, "D0": 4 * P, "WN0": 7 * P,
-                     "WN1": 7 * P, "TT": 7 * P, "DT": P + 16, "H": C * P, "SW": Z0 + 16 + W + PB, "hb": 96,
-                     "u2": 2 * LC, "u1": LC, "vals": PB, "nl": 16, "rows": 384, "ones": 896, "MB": 896, "ME": 528,
-                     "M2": 256, "LS": 144, "NW": 144, "NA": 144, "PN": 1024, "BO": 128, "SC": 128, "tmp": 768,
-                     "base": 512, "QM": 2048, "MX": 640, "crow": PB})):
+SCRATCH = {"AO": ("dram", [N, 128, LC], I32), "AL": ("dram", [N, 128, LC], I32),
+           "DO": ("dram", [N, 128, NL // N], I32), "DL": ("dram", [N, 128, NL // N], I32)}
+for _d, _l in ((I32, {"XI": P, "LI": NL, "DI": NL, "RI": LC, "da": NL, "db": NL, "pi": 8, "pb": 8}),
+               (U16, {"so16": 32, "j16": 2 * NL, "o16": NL, "LU": NL, "LE": N * NL}),
+               (F32, {"YF": P, "YL": N * NL, "hs": 2 * LC, "U": 24, "so": 24, "L": NL, "Lb": NL, "ji": NL, "DD": DAYS * NL,
+                      "pf": 8, "cols": 32, "r16": 144, "zf": 2 * LC, "z0": 24, "NI": 128, "NK": 24}),
+               (BF, {"XO": P, "XL": P, "XE": P, "XS": P, "R2": 2 * LC, "S": 4 * P, "G": 4 * P, "D0": 4 * P, "WN": 7 * P,
+                     "TT0": 7 * P, "TT1": 7 * P, "DT": P + 16, "H": C * P, "SW": Z0 + 16 + W + PB, "hb": 176, "keep": NL,
+                     "u2": 2 * LC, "u1": 2 * LC, "vals": PB, "nl": 16, "rows": 512, "ones": 896, "MB": 896, "ME": 528,
+                     "IDN": 128, "LS": 144, "L2": 144, "L8": 144, "NW": 144, "PN": 1024, "BO": 128, "SC": 128,
+                     "tmp": 896, "base": 512, "QM": 2048, "MX": 1152, "crow": PB})):
     for _k, _n in _l.items():
         SCRATCH[_k] = ("sbuf", [128, _n], _d)
 for _b in range(8):
     SCRATCH["ps%d" % _b] = ("psum", [128, 512], F32)
 
-SEMAPHORES = (["pe", "dve", "act", "pool", "sent", "aux"] + ["sx%d" % i for i in range(N)] + ["ex%d" % i for i in range(N)]
-              + ["el%d" % i for i in range(N)] + ["dm%d" % i for i in range(48)])
+SEMAPHORES = (["pe", "dve", "act", "pool", "sent", "aux", "aud"] + ["sx%d" % i for i in range(N)]
+              + ["ex%d" % i for i in range(N)] + ["el%d" % i for i in range(N)] + ["dm%d" % i for i in range(60)])
 
-CFG = {"cyc": 0.001, "pe": 0.0005, "fix": 0.06, "lat": 0.07, "gat": 1.55, "sca": 3.8, "dma": 2.0, "dbw": 250e3,
-       "hop": (3.0, 5.0), "tch": 6, "rep": 3, "parts": ((0, 640), (640, 1280)), "chunks": ((0, 640), (640, 1280)),
-       "ka": ((0, 1, 2), (0, 1, 2), (0, 1, 2), (0, 1)), "seed": 1, "bias": -0.5, "iters": 2500, "jit": 0.5, "temp": 0.15}
+CFG = {"parts": ((0, 768), (768, 1280)), "chunks": ((0, 768), (768, 1280)), "xfirst": True, "dmafill": ("WN", "TT1"),
+       "cuts": (0, 320, 640, 960, 1280, 1920, 2560, 3200, 3840),
+       "ks": ((0, 1), (1, 2), (2, 3)),
+       "seed": 4, "early": -1.0, "iters": 60000, "soon": 0.1, "temp": 0.0015,
+       "mix": (0.25, 0.5, 0.7, 0.5), "period": 11.0}
+STAGES = {"tot": (-7.2, -6.1), "h": (-6.65, -5.7), "H": (-6.45, -5.55), "Hs": (-6.15, -5.3), "u2": (-6.0, -5.15),
+          "Ix": (-6.7, -6.6, -5.9), "pen": (-5.8, -5.5, -5.0), "xm": (-5.45, -5.1, -4.6), "repWN": (-4.7, -4.1),
+          "u16": (-4.7,), "u1": (-4.62,), "n": (-4.3,), "nl": (-3.65,), "vals": (-3.7, -3.0), "D2": (-3.4,), "Z": (-3.1,),
+          "U": (-3.0,), "so": (-2.75,), "so16": (-2.6,), "scat": (-2.45,), "Ts": (-1.3,), "repTT0": (-0.6,),
+          "repTT1": (-0.6,), "": (-0.6,), "xd": (-5.8, -4.95), "ji": (-1.0,), "j16": (1.95,),
+          "gat": (0.0, 0.0, 1.15, 1.15, 2.3, 3.0), "xs": (2.3, 3.85), "F": (2.0, 3.05, 8.2), "keep": (3.8, 3.95, 9.0),
+          "tg": (3.85, 4.5, 4.9, 6.4, 6.9, 6.95, 8.0, 9.0), "Nb": (4.1, 9.1, 9.2), "N": (7.0, 8.9, 10.1),
+          "Lb": (7.95, 9.7, 10.9), "L": (8.1, 10.0, 11.1), "o16": (9.75, 10.4, 11.3)}
+QUEUES = {"h": "aa", "u2": "dd", "xm": "aad", "u1": "d", "nl": "a", "vals": "-a", "xd": "dd", "ji": "a", "gat": "daadaa",
+          "keep": "aaa", "tg": "aaaaadaa"}
+BASE = {"cyc": 0.9e-3, "pe": 0.5e-3, "mm": 0.004, "fix": 0.055, "lat": 0.07, "gat": 1.55, "sca": 3.8, "dma": 1.2,
+        "bw": 500e3, "row": 0.015, "hold": 0.06, "call": 0.5, "first": 1.2, "rem": 1.2, "xbw": 80e3}
+MODELS = [{}, {"cyc": 1.15e-3, "pe": 0.6e-3, "gat": 1.9, "sca": 2.5, "dma": 1.0, "bw": 600e3, "row": 0.01},
+          {"cyc": 0.85e-3, "pe": 0.45e-3, "gat": 1.15, "sca": 5.0, "dma": 1.5, "bw": 420e3, "row": 0.02, "first": 2.0, "lat": 0.1}]
 STATS = {}
 
 
@@ -60,12 +76,15 @@ def relay_program(g, core, T, topo, s, d):
     dst = T.cores[d]
     rid, pid = topo.addr(dst, core)
     es = topo.engines(core, dst)
+    n = len(topo.engines(T.cores[s], core))
     xs = slice(PB * s, PB * s + PB)
-    for sem, cnt, ap in ((T.sem.aux, 4, T.AL[s]), (T.sem["sx%d" % s], 8, T.XL[:, xs]),
-                         (T.sem["ex%d" % s], 8, T.XE[:, xs]), (T.sem["el%d" % s], 4, T.LL[s])):
+    home = [(T.sem["ex%d" % s], n // 2, T.XE[:, xs]), (T.sem["el%d" % s], n // 2, T.LE[:, NL * s:NL * s + NL])]
+    jobs = [(T.sem.aux, n // 4, T.AL[s]), (T.sem["sx%d" % s], n // 2, T.XL[:, xs]), (T.sem.aud, n // 4, T.DL[s])]
+    jobs += home if CFG["xfirst"] else home[::-1]
+    for sem, cnt, ap in jobs:
         g.wait_ge(sem, cnt)
         g.remote_dma(ap, ap, sem, T.sem.sent, pid, rid, emask(es))
-    g.wait_ge(T.sem.sent, 4 * len(es))
+    g.wait_ge(T.sem.sent, len(jobs) * len(es))
 
 
 def rank_program(g, core, T, topo):
@@ -82,18 +101,20 @@ def rank_program(g, core, T, topo):
     hist = {}
     mcache = {}
 
-    def A(name, lo=0, hi=None, step=1):
+    def A(name, lo=0, hi=None, step=1, part=(0, 128)):
         hi = SCRATCH[name][1][-1] if hi is None else hi
         key = (lo, hi, step)
         if key not in mcache:
             mcache[key] = ((1 << (hi - lo)) - 1) << lo if step == 1 else emask(range(lo, hi, step))
-        ap = T[name][:, lo:hi] if step == 1 else T[name][:, lo:hi:step]
+        ap = T[name][part[0]:part[1], lo:hi] if step == 1 else T[name][part[0]:part[1], lo:hi:step]
         return {"ap": ap, "buf": name, "mask": mcache[key], "n": len(range(lo, hi, step)), "dt": SCRATCH[name][2]}
 
     def slot(name, mask):
         return {"buf": name, "mask": mask}
 
-    def add(var, rd, wr, sem=None, after=(), name=""):
+    today = []
+
+    def add(var, rd, wr, sem=None, after=(), behind=(), name=""):
         i = len(ops)
         pre = {}
         for o, w in [(o, False) for o in rd] + [(o, True) for o in wr]:
@@ -108,12 +129,17 @@ def rank_program(g, core, T, topo):
             lst.append((i, mk, w))
         for j in after:
             pre[j] = True
-        ops.append({"var": var, "pre": pre, "sem": sem, "name": name})
+        for j in behind:
+            pre[j] = pre.get(j, False)
+        kind = ("", i)
+        if today:
+            kind = (name, today.count(name))
+            today.append(name)
+        ops.append({"var": var, "pre": pre, "sem": sem, "name": name, "kind": kind, "day": today[0] if today else None})
         return i
 
     def cyc(n, k=1.0):
-        t = cf["fix"] + max(n * k, 64) * cf["cyc"]
-        return t, t
+        return {"fix": 1, "cyc": max(n * k, 64)}
 
     def narrow(*os_):
         return 0.5 if all(o["dt"] in (BF, U16) for o in os_) else 1.0
@@ -124,69 +150,80 @@ def rank_program(g, core, T, topo):
     def scs(*xs):
         return [x for x in xs if isinstance(x, dict)]
 
+    def activation(out, in0, func, bias, scale):
+        return cyc(out["n"]), lambda q: q.activation(out["ap"], in0["ap"], func, bias=sc(bias), scale=sc(scale))
+
     def ts(out, in0, s1, s2, op0, op1=None, act=None, name=""):
         def f(q):
             if op1 is None:
                 return q.tensor_scalar(out["ap"], in0["ap"], sc(s1), None, op0)
             return q.tensor_scalar(out["ap"], in0["ap"], sc(s1), sc(s2), op0, op1)
-        var = {"dve": cyc(out["n"], narrow(out, in0)) + (f,)}
+        var = {"dve": (cyc(out["n"], narrow(out, in0)), f)}
         if act is not None:
-            var["act"] = cyc(out["n"]) + (lambda q: q.activation(out["ap"], in0["ap"], act[0], bias=sc(act[1]), scale=sc(act[2])),)
-        return add(var, [in0] + scs(s1, s2), [out], name=name)
+            var["act"] = activation(out, in0, *act)
+        return add(var, [in0] + scs(s1, s2) + scs(*(act or ())), [out], name=name)
 
-    def scale(out, in_, s):
-        return ts(out, in_, s, None, ALU.mult, act=(ACTF.Identity, 0.0, s))
+    def scale(out, in_, s, b=0.0, name=""):
+        return ts(out, in_, s, b, ALU.mult, ALU.add, act=(ACTF.Identity, b, s), name=name)
+
+    def sign(out, in_, lo=-1.0, hi=1.0, name=""):
+        return ts(out, in_, lo, hi, ALU.max, ALU.min, act=(ACTF.Sign, 0.0, hi), name=name)
 
     def cp(out, in0, both=True, name=""):
-        var = {"dve": cyc(out["n"], narrow(out, in0)) + (lambda q: q.tensor_copy(out["ap"], in0["ap"]),)}
+        var = {"dve": (cyc(out["n"], narrow(out, in0)), lambda q: q.tensor_copy(out["ap"], in0["ap"]))}
         if both:
-            var["act"] = cyc(out["n"]) + (lambda q: q.activation(out["ap"], in0["ap"], ACTF.Copy),)
+            var["act"] = (cyc(out["n"]), lambda q: q.activation(out["ap"], in0["ap"], ACTF.Copy))
         return add(var, [in0], [out], name=name)
 
     def tt(out, a, b, op, name=""):
         k = 1.0 if (a["buf"].startswith("ps") or b["buf"].startswith("ps")) else 2.0
-        return add({"dve": cyc(out["n"], k) + (lambda q: q.tensor_tensor(out["ap"], a["ap"], b["ap"], op),)}, [a, b], [out], name=name)
+        return add({"dve": (cyc(out["n"], k), lambda q: q.tensor_tensor(out["ap"], a["ap"], b["ap"], op))}, [a, b], [out], name=name)
 
     def ms(out, v):
-        return add({"dve": cyc(out["n"], narrow(out)) + (lambda q: q.memset(out["ap"], v),)}, [], [out])
+        return add({"dve": (cyc(out["n"], narrow(out)), lambda q: q.memset(out["ap"], v))}, [], [out])
 
     def scan(out, d0, d1, init, op0, op1, name=""):
-        return add({"dve": cyc(out["n"], narrow(out, d0, d1)) + (
-            lambda q: q.tensor_tensor_scan(out["ap"], d0["ap"], d1["ap"], sc(init), op0, op1),)}, [d0, d1] + scs(init), [out], name=name)
+        return add({"dve": (cyc(out["n"], narrow(out, d0, d1)), lambda q: q.tensor_tensor_scan(
+            out["ap"], d0["ap"], d1["ap"], sc(init), op0, op1))}, [d0, d1] + scs(init), [out], name=name)
 
     def mm(items, name="", start=True, stop=True):
-        t = sum(max(64, o["n"]) * (4 if r["dt"] == F32 else 1) for o, l, r in items) * cf["pe"]
+        t = sum(max(64, o["n"]) * (4 if r["dt"] == F32 else 1) for o, l, r in items)
 
         def f(q):
             ins = None
             for i, (o, l, r) in enumerate(items):
                 ins = q.matmul(o["ap"], l["ap"], r["ap"], start and i == 0, stop and i == len(items) - 1)
             return ins
-        return add({"pe": (t, t + 0.05, f)}, [x for o, l, r in items for x in (l, r)], [items[0][0]], name=name)
+        return add({"pe": ({"pe": t, "mm": len(items), "tail": 0.05}, f)}, [x for o, l, r in items for x in (l, r)],
+                   [items[0][0]], name=name)
+
+    def iota_call(out, pattern, base, cm):
+        t = {"us": 0.13, "cyc": 2 * out["n"]}
+        if out["dt"] == I32:
+            return t, lambda q: q.iota(out["ap"], pattern, base, cm)
+        return t, lambda q: q.iota(out["ap"], pattern, base, cm, allow_small_or_imprecise_dtypes=True)
 
     def iota(out, pattern, base, cm):
-        t = 0.13 + 2 * out["n"] * cf["cyc"]
-        if out["dt"] == I32:
-            return add({"pool": (t, t, lambda q: q.iota(out["ap"], pattern, base, cm))}, [], [out])
-        return add({"pool": (t, t, lambda q: q.iota(out["ap"], pattern, base, cm, allow_small_or_imprecise_dtypes=True))}, [], [out])
+        return add({"pool": iota_call(out, pattern, base, cm)}, [], [out])
 
     def asel(out, in_, pattern, base, cm):
-        t = 0.17 + 2 * out["n"] * cf["cyc"]
-        return add({"pool": (t, t, lambda q: q.affine_select(out["ap"], in_["ap"], pattern, ALU.is_equal, 0.0, base, cm))}, [in_], [out])
+        return add({"pool": ({"us": 0.17, "cyc": 2 * out["n"]}, lambda q: q.affine_select(
+            out["ap"], in_["ap"], pattern, ALU.is_equal, 0.0, base, cm))}, [in_], [out])
 
     ndma = [0]
 
-    def dmas(jobs, rd, wr, nbytes, qs=("sp", "act"), after=(), name="", hold=0.1):
+    def dmas(jobs, rd, wr, nbytes, rows, qs=("sp", "act"), after=(), name=""):
         sem = T.sem["dm%d" % ndma[0]]
         ndma[0] += 1
 
         def f(q):
             for o, i in jobs:
                 q.dma_start(o, i).then_inc(sem, 16)
-        return add({e: (hold, cf["dma"] + nbytes / cf["dbw"], f) for e in qs}, rd, wr, sem=(sem, 16 * len(jobs)), after=after, name=name)
+        cost = {"hold": len(jobs), "bytes": nbytes, "rows": rows, "dma": 1}
+        return add({e: (cost, f) for e in qs}, rd, wr, sem=(sem, 16 * len(jobs)), after=after, name=name)
 
-    def arrive(sem, cnt, wr, after, lag):
-        return add({"ext": (0.0, lag, None)}, [], wr, sem=(sem, cnt), after=after)
+    def arrive(sem, cnt, wr, after, hops, nbytes):
+        return add({"ext": ({"hops": hops, "far": nbytes}, None)}, [], wr, sem=(sem, cnt), after=after)
 
     others = [d for d in range(N) if d != me]
     via = {d: relays(T, topo, core, T.cores[d]) for d in others}
@@ -194,49 +231,58 @@ def rank_program(g, core, T, topo):
     far = sorted([d for d in others if via[d] is not None], key=lambda d: topo.die(via[d]) == topo.die(core))
     near = [d for d in others if via[d] is None]
     sent = [0]
+    calls = []
 
     def xfer(d, es, src, dst, sem):
         rid, pid = topo.addr(hop[d], core)
         sent[0] += len(es)
         return RemoteDMATransfer(dst_ids=[DstId(rid=rid, pnc=pid)], dma_engine_mask=emask(es), remote_sem=sem, src=src, dst=dst)
 
-    def send(trs, rd, after=()):
-        return add({"pool": (0.5, 0.5, lambda q: q.remote_dma_fused(trs, local_sem=T.sem.sent))}, rd, [], sem="none", after=after, name="send")
+    def send(trs, rd, nbytes):
+        cost = {"call": 1, "first": 0 if calls else 1, "bytes": nbytes * len(trs), "rows": 128 * len(trs), "rem": 1}
+        calls.append(add({"pool": (cost, lambda q: q.remote_dma_fused(trs, local_sem=T.sem.sent))}, rd, [], sem="none",
+                         behind=calls[-1:], name="send"))
+        return calls[-1]
 
-    def send_x(src, land, sem, after=()):
-        e, d, to = topo.engines(core, hop[far[0]]), near[0], T[land][:, PB * me:PB * me + PB]
-        a = send([xfer(f, e[i::2], T[src][:, PB * f:PB * f + PB], to, sem) for i, f in enumerate(far)],
-                 [A(src, PB * f, PB * f + PB) for f in far], after)
-        b = send([xfer(d, topo.engines(core, hop[d]), T[src][:, PB * d:PB * d + PB], to, sem)], [A(src, PB * d, PB * d + PB)], [a])
+    def send_s(src, to, sem, nbytes):
+        e, d = topo.engines(core, hop[far[0]]), near[0]
+        a = send([xfer(f, e[i::2], src(f)["ap"], to, sem) for i, f in enumerate(far)], [src(f) for f in far], nbytes)
+        b = send([xfer(d, topo.engines(core, hop[d]), src(d)["ap"], to, sem)], [src(d)], nbytes)
         return a, b
 
-    def send_d(src, land, sem):
+    def send_d(src, land, sem, nbytes):
         d = near[0]
         e0 = topo.engines(core, hop[d])
         e = [x for x in topo.engines(core, hop[far[0]]) if x not in e0]
         trs = [xfer(f, e[i::2], T[src][f], T[land][me], sem) for i, f in enumerate(far)]
-        return send(trs + [xfer(d, e0, T[src][d], T[land][me], sem)], [slot(src, 15)])
+        return send(trs + [xfer(d, e0, T[src][d], T[land][me], sem)], [slot(src, 15)], nbytes)
 
     def got(s):
         r = relays(T, topo, T.cores[s], core)
         return len(topo.engines(r if r is not None else T.cores[s], core))
 
+    def piece(name):
+        return lambda d: A(name, PB * d, PB * d + PB)
+
+    dmas([(T.AO[:, 0:96, :], T.nb[:]), (T.AO[:, 96:128, :], T.res[:])], [], [slot("AO", 1)], 163840, 32, name="ldl")
     for d in far + near + [me]:
         blk = A("XI", PB * d, PB * d + PB)
-        dmas([(blk["ap"], T.x0[32 * d:32 * d + 32, :])], [], [blk], 128 * PB * 4, name="ldx")
+        dmas([(blk["ap"], T.x0[32 * d:32 * d + 32, :])], [], [blk], 128 * PB * 4, 128, name="ldx")
         cp(A("XL" if d == me else "XO", PB * d, PB * d + PB), blk, both=False, name="cvx")
-    dmas([(T.AO[:, 0:48, :], T.nb[:])], [], [slot("AO", 1)], 122880)
-    dmas([(T.AO[:, 48:96, :], T.dice[:])], [], [slot("AO", 2)], 122880)
-    dmas([(T.AO[:, 96:112, :], T.res[:]), (T.AO[:, 112:128, :], T.res[:])], [], [slot("AO", 4)], 81920, hold=0.2)
-    sl = send_d("AO", "AL", T.sem.aux)
-    sa, sb = send_x("XO", "XL", T.sem["sx%d" % me], [sl])
-    dmas([(T.AL[me], T.AO[me])], [slot("AO", 7)], [slot("AL", 1)], 81920)
+    dmas([(T.DO[:], T.dice[:])], [], [slot("DO", 1)], 122880, 16, name="ldd")
+    sl = send_d("AO", "AL", T.sem.aux, 40960)
+    sa, sb = send_s(piece("XO"), T.XL[:, PB * me:PB * me + PB], T.sem["sx%d" % me], 81920)
+    sd = send_d("DO", "DL", T.sem.aud, 30720)
+    left = arrive(T.sem.sent, sent[0], [], [sl, sa, sb, sd], 0, 0)
+    dmas([(T.AL[me], T.AO[me])], [slot("AO", 1)], [slot("AL", 1)], 40960, 16)
+    dmas([(T.DL[me], T.DO[me])], [slot("DO", 1)], [slot("DL", 1)], 30720, 16)
+    arrive(T.sem.aux, sum(got(s) for s in others), [slot("AL", 2)], [sl], 2.5, 40960)
     for s in near + far:
-        arrive(T.sem["sx%d" % s], got(s), [A("XL", PB * s, PB * s + PB)], [sb if s in near else sa], cf["hop"][0 if s in near else 1])
-    arrive(T.sem.aux, sum(got(s) for s in others), [slot("AL", 2)], [sl], cf["hop"][1])
-    dmas([(T.LI[:], T.AL[:, 0:48, :])], [slot("AL", 3)], [A("LI")], 122880)
-    dmas([(T.DI[:], T.AL[:, 48:96, :])], [slot("AL", 3)], [A("DI")], 122880)
-    dmas([(T.RI[:], T.AL[:, 96:112, :])], [slot("AL", 3)], [A("RI")], 40960)
+        arrive(T.sem["sx%d" % s], got(s), [A("XL", PB * s, PB * s + PB)], [sb if s in near else sa], 0.5 if s in near else 2, 81920)
+    arrive(T.sem.aud, sum(got(s) for s in others), [slot("DL", 2)], [sd], 2, 30720)
+    dmas([(T.LI[:], T.AL[:, 0:96, :])], [slot("AL", 3)], [A("LI")], 122880, 128)
+    dmas([(T.RI[:], T.AL[:, 96:128, :])], [slot("AL", 3)], [A("RI")], 40960, 128)
+    dmas([(T.DI[:], T.DL[:])], [slot("DL", 3)], [A("DI")], 122880, 128)
 
     def mat(name, i):
         return A(name, 128 * i, 128 * i + 128)
@@ -245,17 +291,20 @@ def rank_program(g, core, T, topo):
         return A(name, i, i + 1)
 
     ms(A("ones"), 1.0)
-    ms(A("zf"), 0.0)
-    ms(A("hb"), 0.0)
+    ms(A("zf"), 8.0)
+    ms(A("z0"), 0.0)
+    add({"act": ({"fix": 1, "cyc": 64, "us": 1.3}, lambda q: q.activation(T.hb[:, 0:1], T.ones[:, 0:1], ACTF.Tanh, scale=-16.0))},
+        [col("ones", 0)], [col("hb", 0)])
     iota(col("pi", 0), [[0, 1]], 0, 1)
+    asel(A("IDN"), A("ones", 0, 128), [[1, 128]], 0, -1)
     asel(A("MB"), A("ones"), [[1, 4], [4, 224]], -384, -1)
-    asel(A("M2", 0, 128), A("ones", 0, 128), [[1, 128]], 0, -1)
+    asel(A("ME"), A("ones", 0, 528), [[1, 528]], -3, -4)
     iota(mat("rows", 0), [[0, 8], [1, 16]], 0, 0)
     iota(mat("rows", 1), [[1, 8], [0, 16]], 0, 0)
     iota(mat("rows", 2), [[0, 4], [1, 2], [0, 16]], 0, 0)
+    iota(mat("rows", 3), [[16, 8], [0, 2], [1, 8]], 0, 0)
     iota(A("r16"), [[1, 144]], 0, 0)
     iota(A("crow"), [[1, PB]], -VOFF, 0)
-    asel(A("ME"), A("ones", 0, 528), [[1, 528]], -3, -4)
     p = col("pi", 0)
     ts(col("pb", 0), p, 15, None, ALU.bitwise_and)
     ts(col("pb", 1), p, 4, None, ALU.logical_shift_right)
@@ -263,27 +312,25 @@ def rank_program(g, core, T, topo):
     ts(col("pb", 3), p, 5, None, ALU.logical_shift_right)
     ts(col("pb", 4), p, 7, None, ALU.bitwise_and)
     cp(A("pf", 0, 5), A("pb", 0, 5), both=False)
+    cp(col("pf", 5), p, both=False)
     p16, pg, pc, pq, p8 = [col("pf", i) for i in range(5)]
-    ts(A("cols", 0, 8), A("r16", 0, 8), p8, -256.0, ALU.is_equal, ALU.mult)
-    ts(A("cols", 8, 12), A("r16", 0, 4), pq, None, ALU.is_equal)
+    ts(A("cols", 0, 8), A("r16", 0, 8), p8, -64.0, ALU.is_equal, ALU.mult)
     ts(col("cols", 12), p16, 8.0, None, ALU.is_lt)
     ts(col("cols", 13), p16, 8.0, None, ALU.is_ge)
     ts(col("cols", 14), p16, 15.0, None, ALU.is_equal)
-    e15, thr = col("cols", 14), col("cols", 19)
-    for i, src, a, b in ((15, e15, -255.0, -1.0), (16, e15, 255.0, 1.0),
-                         (17, e15, 16.5, -0.5), (24, e15, 32768.5, -0.5),
-                         (25, e15, 1.0 / 2048 - 16, 16.0),
-                         (18, e15, -1.0 / 128, 1.0 / 128), (26, e15, 1.0, -1.0),
-                         (19, pq, P, -LOFF), (20, pg, 16.0, 15.0), (21, p16, -1.0, -W),
-                         (22, pq, -P, Z0 + 16), (23, pq, -P, Z0 + W // 2)):
-        ts(col("cols", i), src, float(a), float(b), ALU.mult, ALU.add)
-    ts(A("crow"), A("crow"), e15, col("cols", 26), ALU.mult, ALU.add)
-    IDN = mat("M2", 0)
-    if cf["rep"] < N - 1:
-        cp(mat("M2", 1), IDN)
-    ts(A("LS"), A("r16"), col("cols", 20), None, ALU.is_equal)
-    scale(A("NW"), A("LS"), col("cols", 17))
-    scale(A("NA"), A("LS"), col("cols", 24))
+    e15 = col("cols", 14)
+    wgt, tsc, step, own, row15, p21, zone0, jbase, cmul = [col("cols", 15 + i) for i in range(9)]
+    for out, src, a, b in ((wgt, e15, -16.0 * M - 0.5, 0.5),
+                           (tsc, e15, -15, 16),
+                           (step, e15, -1.0 / 128, 1.0 / 128), (own, pq, -P, Z0), (row15, pg, 16, 15), (p21, p16, -1, -W),
+                           (zone0, pq, -P, Z0 + 16), (jbase, pq, P, ROUND - Z0 - W // 2), (cmul, e15, 1.0 / M, 0)):
+        scale(out, src, float(a), float(b))
+    ts(col("cols", 24), e15, -15.0, p16, ALU.mult, ALU.add)
+    scale(A("crow"), A("crow"), cmul, col("cols", 24))
+    IDN = A("IDN")
+    ts(A("LS"), A("r16"), row15, None, ALU.is_equal)
+    scale(A("NW"), A("LS"), wgt)
+    scale(A("L2"), A("LS"), 2.0)
     ts(A("BO"), mat("rows", 1), pg, None, ALU.is_equal)
     ts(A("SC"), mat("rows", 2), pc, None, ALU.is_equal)
     for r in range(8):
@@ -292,51 +339,71 @@ def rank_program(g, core, T, topo):
     ts(mat("tmp", 1), mat("rows", 0), p16, None, ALU.is_le)
     ts(mat("tmp", 2), mat("rows", 0), p16, None, ALU.is_ge)
     ts(mat("tmp", 3), mat("rows", 0), p16, -8192.0, ALU.is_equal, ALU.mult)
-    ts(mat("tmp", 4), mat("rows", 0), 15.0, 2.0, ALU.is_lt, ALU.mult)
-    I1024, I4096, ZERO, HA, HU = [mat("MX", i) for i in range(5)]
-    scale(I1024, IDN, 1024.0)
+    ts(mat("tmp", 4), mat("rows", 0), 15.0, None, ALU.is_lt)
+    E8, I4096, ZERO, HA, HU, TB, NB = [mat("MX", i) for i in range(7)]
+    half = [mat("MX", 7), mat("MX", 8)]
+    for e in range(2):
+        scale(half[e], IDN, col("cols", 12 + e))
+    pk = col("pf", 5)
+    ts(E8, mat("rows", 3), pk, 1024.0, ALU.is_equal, ALU.mult)
+    ts(mat("tmp", 5), mat("rows", 3), pk, None, ALU.is_gt)
+    ts(mat("tmp", 6), mat("rows", 3), pk, col("cols", 12), ALU.is_le, ALU.mult)
+    tt(A("L8", 8, 144), A("L2", 8, 144), A("L2", 0, 136), ALU.add)
     scale(I4096, IDN, 4096.0)
     scale(ZERO, IDN, 0.0)
+    scale(TB, IDN, 1.0, -2.0 * TH / 128)
+    scale(NB, IDN, -7.5, -16.0 * VOFF / 128)
     scale(A("NI"), IDN, -1.0)
-    tt(mat("tmp", 5), mat("tmp", 0), A("BO"), ALU.mult)
-    tt(HA, mat("tmp", 5), I1024, ALU.subtract)
-    tt(HU, mat("tmp", 1), A("BO"), ALU.mult)
+    tt(mat("tmp", 5), mat("tmp", 5), A("BO"), ALU.mult)
+    tt(HA, mat("tmp", 5), E8, ALU.subtract)
+    tt(HU, mat("tmp", 6), A("BO"), ALU.mult)
     tt(mat("tmp", 2), mat("tmp", 2), mat("tmp", 4), ALU.mult)
     for b in range(4):
         tt(mat("base", b), mat("tmp", b), A("SC"), ALU.mult)
+    ts(A("cols", 8, 12), A("r16", 0, 4), pq, None, ALU.is_equal)
     for q in range(N):
         scale(A("QM", 512 * q, 512 * q + 512), A("base"), col("cols", 8 + q))
-    ts(A("NK", 0, 20), A("r16", 0, 20), -16.0, col("cols", 21), ALU.mult, ALU.add)
-    zone, fill = A("SW", Z0, Z0 + P + 16), A("SW", Z0, Z0 + P)
+
+    def ofrank(q, b, src):
+        return mat("QM", 4 * q + b), A(*src)
+
+    ts(A("NK", 0, 20), A("r16", 0, 20), -16.0, p21, ALU.mult, ALU.add)
+    zone = A("SW", Z0, Z0 + P + 16)
     ms(zone, -256.0)
-    flat = cf["rep"] == N - 1
-    own0 = Z0 if flat else 0
-    for name in ["WN0"] * flat + ["TT"]:
+    scale(A("DT"), zone, step)
+
+    def fill(out, v, part=(0, 128), wr=None, qs=("dve", "act", "pool")):
+        src = A("DT", 0, out["n"], part=part)
+        var = {"dve": (cyc(out["n"], 0.5), lambda q: q.memset(out["ap"], float(v))),
+               "act": activation(out, src, ACTF.Identity, float(v), 0.0), "pool": iota_call(out, [[0, out["n"]]], v, 0)}
+        return add({e: var[e] for e in qs}, [src] if "act" in qs else [], [wr or out], name="fill")
+
+    spare = {}
+    for name in ("WN", "TT0", "TT1"):
+        spare[name] = slot(name + "x", 127)
+        parts = [(0, 32 * (N - 1 - b)) if b < N - 1 else (32 * (2 * N - 1 - b), 128) for b in range(2 * N - 1)]
+        if name in cf["dmafill"]:
+            dmas([(T[name][a:z, P * b:P * b + P], T.DT[a:z, 0:P]) for b, (a, z) in enumerate(parts) if b != N - 1],
+                 [A("DT")], [spare[name], A(name, Z0 - 16, Z0)], 983040, 384, qs=("sp",), after=[left], name="dfill")
+            continue
+        for b, part in enumerate(parts):
+            qs = ("pool",)
+            if b in (N - 2, 2 * N - 2):
+                fill(A(name, P * b, P * b + P), 0, qs=qs)
+            elif b != N - 1:
+                fill(A(name, P * b, P * b + P, part=part), 0, part, slot(name + "x", 1 << b), qs)
+    for k, v in enumerate((-1024, 0, 0)):
+        fill(A("D0", k, 4 * P, 4), v, qs=("dve", "act"))
+
+    def spread(name, c0, c1):
         jobs, wr = [], []
         for s in range(1, N):
             cut = 128 - 32 * s
-            for p0, p1, a in ((cut, 128, Z0 + P * s), (0, cut, Z0 + P * (s - N))):
-                jobs.append((T[name][p0:p1, a:a + P], T.SW[p0:p1, Z0:Z0 + P]))
-                wr.append(A(name, a, a + P))
-        dmas(jobs, [fill], wr, 983040, qs=("sp",), after=[sl, sb], hold=983040 / cf["dbw"])
-    for s in range(7 * flat):
-        if s != N - 1:
-            iota(A("WN1", P * s, P * s + P), [[0, P]], 0, 0)
-    scale(A("DT"), zone, col("cols", 18))
-    scale(A("D0", 0, 4 * P, 4), fill, 4.0)
-    for k in (1, 2):
-        scale(A("D0", k, 4 * P, 4), fill, 0.0)
-
-    def spread(name, c0, c1, first, wide):
-        jobs, wr, o = [], [], (Z0 if wide else 0)
-        for s in range(first, N):
-            cut = 128 - 32 * s
-            a, b = (o + P * s, o + P * (s - N)) if wide else (P * s, P * s)
-            jobs += [(T[name][0:cut, a + c0:a + c1], T[name][32 * s:128, o + c0:o + c1]),
-                     (T[name][cut:128, b + c0:b + c1], T[name][0:32 * s, o + c0:o + c1])]
+            a, b = Z0 + P * s, Z0 + P * (s - N)
+            jobs += [(T[name][0:cut, a + c0:a + c1], T[name][32 * s:128, Z0 + c0:Z0 + c1]),
+                     (T[name][cut:128, b + c0:b + c1], T[name][0:32 * s, Z0 + c0:Z0 + c1])]
             wr += [A(name, a + c0, a + c1), A(name, b + c0, b + c1)]
-        nb_ = (N - first) * 256 * (c1 - c0)
-        dmas(jobs, [A(name, o + c0, o + c1)], wr, nb_, qs=("sp",), name="rep" + name, hold=nb_ / cf["dbw"])
+        dmas(jobs, [A(name, Z0 + c0, Z0 + c1)], wr, (N - 1) * 256 * (c1 - c0), (N - 1) * 128, qs=("sp",), name="rep" + name)
 
     def LSr(name, r):
         return A(name, 15 - r, 143 - r)
@@ -357,228 +424,336 @@ def rank_program(g, core, T, topo):
     for j, (b0, b1) in enumerate(((0, 6), (6, 12), (12, 16))):
         for b in range(b0, b1):
             mm([(ps(5 + j, LC * (b - b0), LC * (b - b0 + 1)), mat("PN", b % 8), A("R2", LC * (b // 8), LC * (b // 8 + 1)))])
-        scale(A("D0", 4 * LC * b0 + 3, 4 * LC * b1, 4), ps(5 + j, 0, LC * (b1 - b0)), 1.0 / 256)
-    ts(A("L"), A("LI"), -LOFF, None, ALU.add)
-
-    def offsets():
-        if flat:
-            return ts(A("o16"), A("L"), thr, float(own0), ALU.subtract, ALU.add, name="o16")
-        ts(A("ww"), A("L"), col("cols", 27), float(W), ALU.is_lt, ALU.mult, name="w")
-        tt(A("ww"), A("ww"), A("L"), ALU.add, name="o")
-        return ts(A("o16"), A("ww"), thr, None, ALU.subtract, name="o16")
-
-    if not flat:
-        ts(col("cols", 27), thr, -0.5, None, ALU.add)
-    offsets()
+        scale(A("D0", 4 * LC * b0 + 3, 4 * LC * b1, 4), ps(5 + j, 0, LC * (b1 - b0)), 1.0 / 64, name="res")
+    cp(A("L"), A("LI"), both=False)
+    ts(A("o16"), A("LI"), own, None, ALU.add, name="o16")
+    for t in range(DAYS):
+        src = A("DI")
+        if t:
+            ts(A("da"), src, float(STEP * t), None, ALU.add, name="da")
+            src = A("db")
+            ts(src, A("da"), M - 1, None, ALU.bitwise_and, name="db")
+        ts(A("DD", NL * t, NL * t + NL), src, 1.0 / M, None, ALU.mult, name="dd")
     bank = [0]
 
     def nextbank():
         bank[0] += 1
-        return (bank[0] - 1) % 4
+        return (bank[0] - 1) % 3
 
     for t in range(DAYS):
-        wn = "WN%d" % (t % 2)
-        for p0, p1 in cf["parts"]:
-            c0, c1 = p0 // 16, p1 // 16
-            mm([(ps(4, c0, c1), LSr("LS", r), X(p0 + r, p1, 16)) for r in range(16)], "tot")
-            ts(A("hb", c0 + 1, c1 + 1), ps(4, c0, c1), float(TH), None, ALU.is_ge, name="h")
-            o = ps(4, 96 + c0, 96 + c1)
-            mm([(o, HA, A("hb", c0 + 1, c1 + 1)), (o, HU, A("hb", c0, c1)), (o, I1024, A("hb", c0, c1))], "H")
-            scan(A("hs", c0, c1), o, A("zf", c0, c1), col("hs", c0 - 1) if c0 else 0.0, ALU.add, ALU.add, name="Hs")
-            for e in range(2):
-                ts(A("u2", 2 * c0 + e, 2 * c1, 2), A("hs", c0, c1), float(CAP - 1024), col("cols", 12 + e), ALU.is_ge, ALU.mult, name="u2")
+        today[:] = [t]
+        tn, un = "TT%d" % (t % 2), LC * (t % 2)
+        for pi_, (p0, p1) in enumerate(cf["parts"]):
+            c0, c1, pb = p0 // 8, p1 // 8, 3 + pi_ % 2
+            o = ps(pb, c0, c1)
+            mm([(o, TB, A("ones", c0, c1))] + [(o, LSr("L8", r), X(p0 + r, p1, 8)) for r in range(8)], "tot")
+            sign(A("hb", c0 + 1, c1 + 1), o, name="h")
+            o = ps(pb, 2 * LC + c0, 2 * LC + c1)
+            mm([(o, HA, A("hb", c0 + 1, c1 + 1)), (o, HU, A("hb", c0, c1)), (o, E8, A("hb", c0, c1))], "H")
+            scan(A("hs", c0, c1), o, A("zf", c0, c1), col("hs", c0 - 1) if c0 else float(2 * (1024 - CAP) + 1), ALU.add, ALU.add, name="Hs")
+            sign(A("u2", c0, c1), A("hs", c0, c1), name="u2")
             k = -(-(p1 - p0) // 512)
             n = (p1 - p0) // k
-            own = [(nextbank(), p0 + n * i) for i in range(k)]
-            for b, lo in own:
+            mine = [(nextbank(), p0 + n * i) for i in range(k)]
+            for b, lo in mine:
                 mm([(ps(b, 0, n), IDN, X(lo, lo + n))], "Ix", True, False)
-            for b, lo in own:
+            for b, lo in mine:
                 mm([(ps(b, r, n, 8), mat("PN", r), A("u2", lo // 8, (lo + n) // 8)) for r in range(8)], "pen", False, True)
-                cp(A(wn, own0 + lo, own0 + lo + n), ps(b, 0, n), name="xm")
-            if cf["rep"]:
-                spread(wn, p0, p1, N - cf["rep"], flat)
-            for _, lo in own:
-                for s in range(1, N - cf["rep"]):
-                    b = nextbank()
-                    mm([(ps(b, 0, n), A("M2", 32 * s, 32 * s + 128), A(wn, lo, lo + n))], "perm")
-                    cp(A(wn, P * s + lo, P * s + lo + n), ps(b, 0, n), name="win")
-        ts(A("u1"), A("hs"), float(CAP - 1024), None, ALU.is_ge, name="u1")
+                scale(A("WN", Z0 + lo, Z0 + lo + n), ps(b, 0, n), 1.0, -128.0, name="xm")
+            spread("WN", p0, p1)
+        u1 = A("u1", un, un + LC)
+        mm([(ps(5, PB, PB + LC), half[e], A("u2", e, 2 * LC, 2)) for e in range(2)], "u16")
+        cp(u1, ps(5, PB, PB + LC), name="u1")
         for p0, p1 in cf["chunks"]:
             ts(A("G", 4 * p0 + 3, 4 * p1, 4), X(p0, p1), float(-DEC), 0.0, ALU.add, ALU.max,
                act=(ACTF.Relu, float(-DEC), 1.0), name="xd")
-        mm([(ps(5, 0, 5), LSr("LS", r), A("u1", r, LC, 16)) for r in range(16)], "n")
+        mm([(ps(3, 352, 357), LSr("LS", r), A("u1", un + r, un + LC, 16)) for r in range(16)], "n")
         nl = A("nl", 0, 5)
-        cp(nl, ps(5, 0, 5), name="nl")
-        mm([(ps(5, 32, 53), ZERO, A("ones", 0, 21))]
-           + [(ps(5, 32 + 5 * q, 37 + 5 * q), mat("QM", 4 * q), nl) for q in range(N)]
-           + [(ps(5, 33 + 5 * q, 38 + 5 * q), mat("QM", 4 * q + 1), nl) for q in range(N)], "D2")
-        mm([(ps(5, 64, 84), A("NI"), A("NK", 0, 20))]
-           + [(ps(5, 64 + 5 * q, 69 + 5 * q), mat("QM", 4 * q + 3), nl) for q in range(N)], "Z")
-        scan(A("U", 0, 21), ps(5, 32, 53), A("zf", 0, 21), 0.0, ALU.add, ALU.add, name="U")
-        tt(A("so", 0, 20), A("U", 0, 20), ps(5, 64, 84), ALU.max, name="so")
+        scale(nl, ps(3, 352, 357), 0.5, 8.0, name="nl")
+        mm([(ps(3, 384, 405), ZERO, A("ones", 0, 21))]
+           + [(ps(3, 384 + 5 * q, 389 + 5 * q),) + ofrank(q, 0, ("nl", 0, 5)) for q in range(N)]
+           + [(ps(3, 385 + 5 * q, 390 + 5 * q),) + ofrank(q, 1, ("nl", 0, 5)) for q in range(N)], "D2")
+        mm([(ps(4, 352, 372), A("NI"), A("NK", 0, 20))]
+           + [(ps(4, 352 + 5 * q, 357 + 5 * q),) + ofrank(q, 3, ("nl", 0, 5)) for q in range(N)], "Z")
+        scan(A("U", 0, 21), ps(3, 384, 405), A("z0", 0, 21), 0.0, ALU.add, ALU.add, name="U")
+        tt(A("so", 0, 20), A("U", 0, 20), ps(4, 352, 372), ALU.max, name="so")
         sw, so16, vals = A("SW"), A("so16", 0, 20), A("vals")
-        ts(so16, A("so", 0, 20), col("cols", 22), None, ALU.add, name="so16")
-        mm([(ps(4, 192, 192 + PB), IDN, A("crow"))]
-           + [(ps(4, 192 + LC * q, 192 + LC * (q + 1)), mat("QM", 4 * q + 2), A("u1")) for q in range(N)], "vals")
-        cp(vals, ps(4, 192, 192 + PB), name="vals")
-        add({"dve": cyc(PB, cf["sca"]) + (lambda q: q.tensor_copy(sw["ap"].indirect(so16["ap"]), vals["ap"]),)},
+        ts(so16, A("so", 0, 20), zone0, None, ALU.add, name="so16")
+        mm([(ps(5, 0, PB), IDN, A("crow"))]
+           + [(ps(5, LC * q, LC * (q + 1)),) + ofrank(q, 2, ("u1", un, un + LC)) for q in range(N)], "vals")
+        cp(vals, ps(5, 0, PB), name="vals")
+        add({"dve": ({"fix": 1, "sca": PB}, lambda q: q.tensor_copy(sw["ap"].indirect(so16["ap"]), vals["ap"]))},
             [so16, vals], [sw], name="scat")
-        scan(A("TT", Z0 - 16, Z0 + P), A("DT"), zone, -256.0, ALU.add, ALU.max, name="Ts")
-        spread("TT", 0, P, 1, True)
+        scan(A(tn, Z0 - 16, Z0 + P), A("DT"), zone, -256.0, ALU.add, ALU.max, name="Ts")
+        spread(tn, 0, P)
         if t < DAYS - 1:
             iota(zone, [[0, P + 16]], -256, 0)
-        if t > 0:
-            ts(A("da"), A("DI"), float(STEP), None, ALU.add, name="da")
-            ts(A("DI"), A("da"), M - 1, None, ALU.bitwise_and, name="db")
-        scale(col("U", 21), col("U", 20), 1.0 / M)
-        ts(A("ji"), A("DI"), col("U", 21), -(W / 2 + 0.5 - 0.5 / M), ALU.mult, ALU.add, name="ji")
-        ts(A("j16"), A("ji"), col("cols", 23), None, ALU.add, name="j16")
-        win = A(wn, 0, 7 * P if flat else W)
+        scale(A("ji"), A("DD", NL * t, NL * t + NL), col("U", 20), -(W / 2 + 0.5 - 0.5 / M), name="ji")
+        ts(A("j16", NL * (t % 2), NL * (t % 2 + 1)), A("ji"), ROUND, jbase, ALU.add, ALU.subtract, name="j16")
+        win = A("WN")
         for p0, p1 in cf["chunks"]:
-            n = p1 - p0
+            cost = {"fix": 1, "gat": p1 - p0}
             for k in range(C):
                 o = A("G", 4 * p0 + k, 4 * p1, 4)
                 off = A("o16", LC * k + p0 // 16, LC * k + p1 // 16)
-                add({"dve": cyc(n, cf["gat"]) + (lambda q, o=o, off=off, win=win: q.tensor_copy(o["ap"], win["ap"].indirect(off["ap"])),),
-                     "act": cyc(n, cf["gat"]) + (lambda q, o=o, off=off, win=win: q.activation(o["ap"], win["ap"].indirect(off["ap"]), ACTF.Copy),)},
-                    [win, off], [o], name="gat")
+                add({"dve": (cost, lambda q, o=o, off=off: q.tensor_copy(o["ap"], win["ap"].indirect(off["ap"]))),
+                     "act": (cost, lambda q, o=o, off=off: q.activation(o["ap"], win["ap"].indirect(off["ap"]), ACTF.Copy))},
+                    [win, spare["WN"], off], [o], name="gat")
             scan(A("S", 4 * p0, 4 * p1), A("D0", 4 * p0, 4 * p1), A("G", 4 * p0, 4 * p1), 0.0, ALU.add, ALU.max, name="xs")
-        tab, lo_, hi_, tsc = A("TT"), col("cols", 15), col("cols", 16), col("cols", 25)
-        n = C * P // cf["tch"]
-        for h in range(cf["tch"]):
-            o, off = A("H", n * h, n * h + n), A("j16", n // 16 * h, n // 16 * (h + 1))
-            if h * C // cf["tch"] in cf["ka"][t]:
-                add({"act": cyc(n, cf["gat"]) + (lambda q, o=o, off=off: q.activation(
-                    o["ap"], tab["ap"].indirect(off["ap"]), ACTF.Tanh, scale=tsc["ap"]),)}, [tab, off, tsc], [o], name="tga")
-            else:
-                add({"dve": cyc(n, cf["gat"]) + (lambda q, o=o, off=off: q.tensor_scalar(
-                    o["ap"], tab["ap"].indirect(off["ap"]), lo_["ap"], hi_["ap"], ALU.max, ALU.min),)}, [tab, off, lo_, hi_], [o], name="tg")
-        mm([(ps(7, 0, NL), A("NI"), A("L"))], "negL", True, False)
-        for k in range(C):
-            mm([(ps(7, LC * k, LC * k + LC), LSr("NA" if k in cf["ka"][t] else "NW", r), A("H", P * k + r, P * k + P, 16))
-                for r in range(16)], "N", False, k == C - 1)
-        for k in range(C):
-            o = ps(6, LC * k, LC * k + LC)
-            mm([(o, I4096, A("u1"))] + [(o, LSr("LS", r), A("G", 4 * r + k, 4 * P, 64)) for r in range(16)], "F")
-        ts(A("mm"), ps(6, 0, NL), 5000.0, None, ALU.is_gt, name="m")
-        tt(A("tt"), ps(7, 0, NL), A("mm"), ALU.mult, name="t")
-        if t == DAYS - 1:
-            ts(A("Lp"), A("L"), LOFF, None, ALU.add, act=(ACTF.Identity, LOFF, 1.0))
-            tt(A("Lp"), A("Lp"), A("tt"), ALU.add, name="Lf")
-            ts(A("Lf"), A("Lp"), 12582912.0, -12582912.0, ALU.add, ALU.add, name="round")
-        else:
-            tt(A("L"), A("L"), A("tt"), ALU.add, name="L")
-            offsets()
+        for h0, h1 in zip(cf["cuts"], cf["cuts"][1:]):
+            o, tab, cost = A("H", h0, h1), A(tn), {"fix": 1, "gat": h1 - h0}
+            off = A("j16", NL * (t % 2) + h0 // 16, NL * (t % 2) + h1 // 16)
+            got_ = tab["ap"].indirect(off["ap"])
+            add({"act": (cost, lambda q, o=o, x=got_: q.activation(o["ap"], x, ACTF.Tanh, scale=tsc["ap"])),
+                 "dve": (cost, lambda q, o=o, x=got_: q.tensor_scalar(o["ap"], x, -1.0, 1.0, ALU.max, ALU.min))},
+                [tab, spare[tn], off, tsc], [o], name="tg")
+        for i, (k0, k1) in enumerate(cf["ks"]):
+            for k in range(k0, k1):
+                o = ps(6 + min(i, 1), LC * k, LC * k + LC)
+                mm([(o, I4096, u1)] + [(o, LSr("L2", r), A("G", 4 * r + k, 4 * P, 64)) for r in range(16)], "F")
+            ts(A("keep", LC * k0, LC * k1), ps(6 + min(i, 1), LC * k0, LC * k1), 5500.0, 16384.0, ALU.is_lt, ALU.mult,
+               act=(ACTF.Relu, 44000.0, -8.0), name="keep")
+        for i, (k0, k1) in enumerate(cf["ks"]):
+            a, b, pb = LC * k0, LC * k1, 6 + i % 2
+            mm([(ps(pb, NL + a, NL + b), NB, A("ones", a, b)), (ps(pb, NL + a, NL + b), IDN, A("keep", a, b))], "Nb", True, False)
+            for k in range(k0, k1):
+                mm([(ps(pb, NL + LC * k, NL + LC * k + LC), LSr("NW", r), A("H", P * k + r, P * k + P, 16)) for r in range(16)],
+                   "N", False, k == k1 - 1)
+            tt(A("Lb", a, b), ps(pb, NL + a, NL + b), A("L", a, b), ALU.min, name="Lb")
+            add({"act": activation(A("L", a, b), A("Lb", a, b), ACTF.Abs, 0.0, 1.0)}, [A("Lb", a, b)], [A("L", a, b)], name="L")
+            if t < DAYS - 1:
+                ts(A("o16", a, b), A("L", a, b), own, None, ALU.add, name="o16")
 
-    for d in far + near + [me]:
-        b = nextbank()
+    today[:] = []
+    for b, d in enumerate(far + near + [me]):
         for j in range(4):
             mm([(ps(b, 0, PB), A("ME", 128 * d - j + 3, 128 * d - j + 131), X(PB * j, PB * j + PB))], "back", j == 0, j == 3)
         cp(A("YF" if d == me else "XS", PB * d, PB * d + PB), ps(b, 0, PB), name="out")
-    sa, sb = send_x("XS", "XE", T.sem["ex%d" % me])
-    dmas([(T.LD[:], T.Lf[:])], [A("Lf")], [slot("LD", 15)], 122880)
-    sl = send_d("LD", "LL", T.sem["el%d" % me])
-    dmas([(T.ynb[32 * me:32 * me + 32, :], T.Lf[32 * me:32 * me + 32, :])], [A("Lf")], [], 30720)
+    cp(A("LU"), A("L"), both=False, name="lu")
+    home = [lambda: send_s(piece("XS"), T.XE[:, PB * me:PB * me + PB], T.sem["ex%d" % me], 81920),
+            lambda: send_s(lambda d: A("LU"), T.LE[:, NL * me:NL * me + NL], T.sem["el%d" % me], 61440)]
+    if cf["xfirst"]:
+        sx, sl = home[0](), home[1]()
+    else:
+        sl, sx = home[1](), home[0]()
+    rows = (32 * me, 32 * me + 32)
+    dmas([(T.ynb[32 * me:32 * me + 32, :], T.L[32 * me:32 * me + 32, :])], [A("L")], [], 30720, 32)
     blk = A("YF", PB * me, PB * me + PB)
-    dmas([(T.yx[32 * me:32 * me + 32, :], blk["ap"])], [blk], [], 163840)
+    dmas([(T.yx[32 * me:32 * me + 32, :], blk["ap"])], [blk], [], 163840, 128)
     for s in near + far:
-        lag = cf["hop"][0 if s in near else 1]
+        i, hops = (1, 0.5) if s in near else (0, 1.5)
         land, blk = A("XE", PB * s, PB * s + PB), A("YF", PB * s, PB * s + PB)
-        arrive(T.sem["ex%d" % s], got(s), [land], [sb if s in near else sa], lag)
+        arrive(T.sem["ex%d" % s], got(s), [land], [sx[i]], hops, 81920)
         cp(blk, land, name="cvy")
-        dmas([(T.yx[32 * s:32 * s + 32, :], blk["ap"])], [blk], [], 163840)
-        arrive(T.sem["el%d" % s], got(s), [slot("LL", 1 << s)], [sl, sb], lag)
-        dmas([(T.ynb[32 * s:32 * s + 32, :], T.LL[s])], [slot("LL", 1 << s)], [], 30720)
+        dmas([(T.yx[32 * s:32 * s + 32, :], blk["ap"])], [blk], [], 163840, 128, name="stx")
+        land, blk = A("LE", NL * s, NL * s + NL, part=rows), A("YL", NL * s, NL * s + NL, part=rows)
+        arrive(T.sem["el%d" % s], got(s), [land], [sl[i]], hops, 61440)
+        cp(blk, land, both=False, name="cvl")
+        dmas([(T.ynb[32 * s:32 * s + 32, :], blk["ap"])], [blk], [], 30720, 32, name="stl")
 
     n = len(ops)
+    pres = [[(j, w or ops[j]["sem"] not in (None, "none")) for j, w in o["pre"].items()] for o in ops]
+    above = [0] * n
+    for i in range(n):
+        for j, w in pres[i]:
+            above[i] |= above[j] | 1 << j
+        pres[i] = [(j, w) for j, w in pres[i] if not any(above[k] >> j & 1 for k, _ in pres[i])]
     succ = [[] for _ in ops]
-    for i, o in enumerate(ops):
-        for j in o["pre"]:
-            succ[j].append(i)
-    lat = cf["lat"]
+    for i in range(n):
+        for j, w in pres[i]:
+            succ[j].append((i, w))
+
+    def order(key):
+        return sorted(range(n), key=lambda i: (key[i], i))
+
+    def times(c, m):
+        x = lambda k: c.get(k, 0)
+        hold = (x("fix") * m["fix"] + (x("cyc") + x("gat") * m["gat"] + x("sca") * m["sca"]) * m["cyc"] + x("pe") * m["pe"]
+                + x("mm") * m["mm"] + x("us") + x("hold") * m["hold"] + x("call") * m["call"] + x("first") * m["first"])
+        if "bytes" in c:
+            wait = x("dma") * m["dma"] + x("rem") * m["rem"]
+            return hold, x("first") * m["first"] + 0.6 * wait, x("bytes") / m["bw"] + x("rows") * m["row"] / 16, 0.4 * wait
+        return hold, hold, 0.0, x("tail") + x("hops") * m["rem"] + x("far") / m["xbw"]
+
+    tms = []
+    for d in MODELS:
+        m = dict(BASE, **d)
+        tms.append((m["lat"], [{e: times(v[0], m) for e, v in o["var"].items()} for o in ops]))
 
     def place(line, lo, busy):
-        for k, (a, b) in enumerate(line):
-            if lo + busy <= a + 1e-9:
-                return lo, k
-            lo = max(lo, b)
-        return lo, len(line)
+        k = len(line)
+        while k and line[k - 1][1] > lo:
+            k -= 1
+        while k < len(line) and lo + busy > line[k][0] + 1e-9:
+            lo = max(lo, line[k][1])
+            k += 1
+        return lo, k
 
-    def forward(key, bias):
-        start, eng = [0.0] * n, [None] * n
-        lines = {e: [] for e in Q}
-        left = [len(o["pre"]) for o in ops]
-        ready = [i for i in range(n) if left[i] == 0]
-        while ready:
-            i = min(ready, key=lambda x: key[x])
-            ready.remove(i)
+    def forward(key, bias, model):
+        lat, tm = tms[model]
+        start, held, done, eng = [0.0] * n, [0.0] * n, [0.0] * n, [None] * n
+        lines = {e: [] for e in list(Q) + ["dq"]}
+        key = list(key)
+        for i in range(n):
+            for j, w in pres[i]:
+                if key[j] > key[i]:
+                    key[i] = key[j]
+        for i in order(key):
             best = None
-            for e, v in ops[i]["var"].items():
+            for e, v in tm[i].items():
                 lo, k = 0.0, 0
-                for j, w in ops[i]["pre"].items():
-                    u = ops[j]["var"][eng[j]]
-                    lo = max(lo, start[j] + (u[1] + lat if (eng[j] != e or w or ops[j]["sem"] is not None) else u[0]))
+                for j, w in pres[i]:
+                    x = done[j] if (w or eng[j] != e) else held[j]
+                    if x > lo:
+                        lo = x
                 if e != "ext":
                     lo, k = place(lines[e], lo, v[0])
-                f = lo + v[1] + (bias[i] if e == "dve" else 0.0)
+                f = lo + v[0] + (bias[i] if e == "dve" else 0.0)
                 if best is None or f < best[0]:
                     best = (f, lo, e, k)
-            _, start[i], eng[i], k = best
-            if eng[i] != "ext":
-                lines[eng[i]].insert(k, (start[i], start[i] + ops[i]["var"][eng[i]][0]))
-            for j in succ[i]:
-                left[j] -= 1
-                if left[j] == 0:
-                    ready.append(j)
-        return max(start[i] + ops[i]["var"][eng[i]][1] for i in range(n)), start, eng
+            _, lo, e, k = best
+            v = tm[i][e]
+            start[i], held[i], eng[i] = lo, lo + v[0], e
+            if e != "ext":
+                lines[e].insert(k, (lo, lo + v[0]))
+            x = lo + v[1]
+            if v[2]:
+                x, k = place(lines["dq"], x, v[2])
+                lines["dq"].insert(k, (x, x + v[2]))
+            done[i] = x + v[2] + v[3] + lat
+        return start, done, eng
 
-    def backward(start, eng):
-        r = [0.0] * n
-        lines = {e: [] for e in Q}
-        left = [len(x) for x in succ]
-        ready = [i for i in range(n) if left[i] == 0]
-        while ready:
-            j = max(ready, key=lambda x: start[x] + ops[x]["var"][eng[x]][1])
-            ready.remove(j)
-            u = ops[j]["var"][eng[j]]
-            lo = u[1] - u[0]
-            for i in succ[j]:
-                c = u[1] + lat if (eng[j] != eng[i] or ops[i]["pre"][j] or ops[j]["sem"] is not None) else u[0]
-                lo = max(lo, r[i] + ops[i]["var"][eng[i]][0] + c - u[0])
-            if eng[j] != "ext":
-                lo, k = place(lines[eng[j]], lo, u[0])
-                lines[eng[j]].insert(k, (lo, lo + u[0]))
-            r[j] = lo
-            for i in ops[j]["pre"]:
-                left[i] -= 1
-                if left[i] == 0:
-                    ready.append(i)
-        return [-(r[i] + ops[i]["var"][eng[i]][0]) for i in range(n)]
+    def replay(seq, eng, model, was=None, first=0):
+        lat, tm = tms[model]
+        free, last = dict.fromkeys(list(Q) + ["ext"], 0.0), dict.fromkeys(list(Q) + ["ext", "dq"])
+        dq = 0.0
+        if was is None:
+            held, done, why = [0.0] * n, [0.0] * n, [None] * n
+        else:
+            held, done, why = was[2][:], was[3][:], was[4][:]
+            for i in seq[first - 1::-1] if first else ():
+                e = eng[i]
+                if last[e] is None and e != "ext":
+                    free[e], last[e] = held[i], i
+                if last["dq"] is None and tm[i][e][2]:
+                    dq, last["dq"] = done[i] - lat - tm[i][e][3], i
+                if None not in (last["pe"], last["dve"], last["act"], last["pool"], last["sp"], last["dq"]):
+                    break
+        for i in seq[first:]:
+            e = eng[i]
+            lo, y = free[e], None
+            for j, w in pres[i]:
+                x = done[j] if (w or eng[j] != e) else held[j]
+                if x >= lo:
+                    lo, y = x, j
+            v = tm[i][e]
+            why[i] = (y, False) if y is not None else (last[e], True)
+            held[i] = lo + v[0]
+            if e != "ext":
+                free[e], last[e] = held[i], i
+            x = lo + v[1]
+            if v[2]:
+                if dq > x:
+                    x, why[i] = dq, (last["dq"], True)
+                x = dq = x + v[2]
+                last["dq"] = i
+            done[i] = x + v[3] + lat
+        span = max(done)
+        i, path = done.index(span), []
+        while i is not None:
+            j, queue = why[i]
+            if queue and j is not None:
+                path.append((j, i))
+            i = j
+        return span, path, held, done, why
+
+    def shift(seq, i, j):
+        a, b = seq.index(j), seq.index(i)
+        if a > b or above[i] >> j & 1:
+            return None
+        mid = seq[a:b + 1]
+        up = [x for x in mid if x == i or above[i] >> x & 1]
+        return seq[:a] + up + [x for x in mid if not (x == i or above[i] >> x & 1)] + seq[b + 1:]
+
+    def sink(seq, j, i):
+        a, b = seq.index(j), seq.index(i)
+        if a > b or above[i] >> j & 1:
+            return None
+        mid = seq[a:b + 1]
+        down = [x for x in mid if x == j or above[x] >> j & 1]
+        return seq[:a] + [x for x in mid if not (x == j or above[x] >> j & 1)] + down + seq[b + 1:]
 
     if "plan" not in STATS:
         rng = np.random.default_rng(cf["seed"])
-        prio = [0.0] * n
+        key, bias = [1e9] * n, [0.0] * n
         for i in range(n - 1, -1, -1):
-            prio[i] = min(v[1] for v in ops[i]["var"].values()) + lat + max([prio[j] for j in succ[i]] + [0.0])
-        key, bias = [-x for x in prio], [cf["bias"]] * n
-        best = cur = None
+            name, k = ops[i]["kind"]
+            if ops[i]["day"] is not None:
+                key[i] = cf["period"] * ops[i]["day"] + STAGES[name][k]
+                bias[i] = {"a": 9.0, "d": -9.0, "-": 0.0}[QUEUES.get(name, "------")[k]]
+            elif succ[i]:
+                key[i] = min(key[j] for j, w in succ[i]) - min(sum(v[1:]) for v in tms[0][1][i].values())
+                key[i] = min(key[i], cf["early"]) if ops[i]["name"] in ("da", "db", "dd", "fill") else key[i]
+            else:
+                key[i] = cf["period"] * (DAYS + 1)
+        start, done, eng = forward(key, bias, 0)
+        seq = order(start)
+        twin = {(o["kind"], o["day"]): i for i, o in enumerate(ops)}
+        best = cur = unit = None
         for it in range(cf["iters"]):
-            span, start, eng = forward(key, bias)
-            if best is None or span <= best[0]:
-                best = (span, key, bias)
-            if cur is None or span <= cur[0] + cf["temp"] * (1 - it / cf["iters"]) * float(rng.random()):
-                cur = (span, key, bias, backward(start, eng))
-            a = float(rng.random()) * span
-            key = [x + (cf["jit"] * float(y) if a - 8 < x + span < a + 8 else 0.0) for x, y in zip(cur[3], rng.random(n))]
-            bias = [b if y > 0.03 else 4 * float(z) - 2 for b, y, z in zip(cur[2], rng.random(n), rng.random(n))]
+            if seq is not None:
+                first = 0
+                while cur and first < n and seq[first] == cur[1][first] and eng[seq[first]] == cur[2][seq[first]]:
+                    first += 1
+                runs = [replay(seq, eng, m, cur and cur[5][m], first) for m in range(len(tms))]
+                unit = unit or [r[0] for r in runs]
+                score = sum((r[0] + cf["soon"] * sum(r[3]) / n) / u for r, u in zip(runs, unit)) / len(unit)
+                if best is None or score <= best[0]:
+                    best = (score, seq, eng, [r[0] for r in runs])
+                if cur is None or score <= cur[0] - cf["temp"] * (1 - it / cf["iters"]) * float(np.log(rng.random())):
+                    cur = (score, seq, eng, [x for r in runs for x in r[1]], runs[0][2], runs)
+            seq, eng, how = cur[1], cur[2], float(rng.random())
+            j, i = cur[3][int(rng.integers(len(cur[3])))]
+            if it % 50 == 0:
+                seq = order([cur[4][x] - tms[0][1][x][eng[x]][0] for x in range(n)])
+                continue
+            if how >= cf["mix"][2]:
+                x = int(rng.integers(n))
+                line = [y for y in seq if eng[y] == eng[x]]
+                k = line.index(x)
+                y = min(max(k + int(rng.integers(-5, 6)), 0), len(line) - 1)
+                j, i, how = (line[y], x, 0.0) if y < k else (x, line[y], cf["mix"][0])
+            pairs = [(j, i)]
+            if rng.random() < cf["mix"][3] and ops[j]["day"] is not None and ops[i]["day"] is not None:
+                pairs = [(twin.get((ops[j]["kind"], ops[j]["day"] + d)), twin.get((ops[i]["kind"], ops[i]["day"] + d)))
+                         for d in range(1 - DAYS, DAYS)]
+                pairs = [x for x in pairs if None not in x]
+            if how < cf["mix"][1]:
+                for j, i in pairs:
+                    seq = (shift(seq, i, j) if how < cf["mix"][0] else sink(seq, j, i)) or seq
+                seq = None if seq is cur[1] else seq
+            else:
+                side = int(rng.integers(2))
+                x = (j, i)[side]
+                can = [e for e in ops[x]["var"] if e != eng[x]]
+                if can:
+                    eng, e = list(eng), can[int(rng.integers(len(can)))]
+                    for y in pairs:
+                        eng[y[side]] = e
+                else:
+                    seq = None
         STATS["plan"] = best
-    span, start, eng = forward(STATS["plan"][1], STATS["plan"][2])
-    seq = sorted(range(n), key=lambda i: (start[i], i))
-    STATS[me] = (span, [(start[i], start[i] + ops[i]["var"][eng[i]][1], eng[i], ops[i]["name"]) for i in seq])
+    seq, eng = STATS["plan"][1:3]
+    span, path, held, done, why = replay(seq, eng, 0)
+    STATS[me] = (span, [(held[i] - tms[0][1][i][eng[i]][0], done[i], eng[i], ops[i]["name"]) for i in seq])
 
     def needs(i):
         return [j for j, w in ops[i]["pre"].items() if ops[j]["sem"] != "none" and (eng[j] != eng[i] or w or ops[j]["sem"] is not None)]
 
+    mine = [i for i in seq if eng[i] == "pool" and ops[i]["sem"] is None]
+    for a, b in zip(mine, mine[1:]):
+        if "fill" in (ops[a]["name"], ops[b]["name"]):
+            ops[b]["pre"][a] = True
     pos = {}
     seen = {e: {} for e in Q}
     wanted = set()
@@ -616,7 +791,7 @@ def rank_program(g, core, T, topo):
             if v > seen[e].get(f, 0):
                 seen[e][f] = v
                 q.wait_ge(T.sem[f], v)
-        ins = ops[i]["var"][e][2](q)
+        ins = ops[i]["var"][e][1](q)
         if i in wanted:
             count[e] += 1
             val[i] = count[e]

import numpy as np
from concourse.bass import DstId, RemoteDMATransfer
from concourse.mybir import AluOpType, ActivationFunctionType

ALU = AluOpType
ACTF = ActivationFunctionType
N, P, C, CAP, TH, DAYS, BITS, DEC, STEP = 4, 1280, 3, 448, 1440, 4, 11, 8, 77
W = N * P
M = 1 << BITS
PB = P // N
LC = P // 16
NL = C * LC
Z0 = (N - 1) * P
VOFF = 160
ROUND = 12582912.0

BF, F32, I32, U16 = "bfloat16", "float32", "int32", "uint16"
SCRATCH = {"AO": ("dram", [N, 128, LC], I32), "AL": ("dram", [N, 128, LC], I32),
           "DO": ("dram", [N, 128, NL // N], I32), "DL": ("dram", [N, 128, NL // N], I32)}
for _d, _l in ((I32, {"XI": P, "LI": NL, "DI": NL, "RI": LC, "da": NL, "db": NL, "pi": 8, "pb": 8}),
               (U16, {"so16": 32, "j16": 2 * NL, "o16": NL, "LU": NL, "LE": N * NL}),
               (F32, {"YF": P, "YL": N * NL, "hs": 2 * LC, "U": 24, "so": 24, "L": NL, "Lb": NL, "ji": NL, "DD": DAYS * NL,
                      "pf": 8, "cols": 32, "r16": 144, "zf": 2 * LC, "z0": 24, "NI": 128, "NK": 24}),
               (BF, {"XO": P, "XL": P, "XE": P, "XS": P, "R2": 2 * LC, "S": 4 * P, "G": 4 * P, "D0": 4 * P, "WN": 7 * P,
                     "TT0": 7 * P, "TT1": 7 * P, "DT": P + 16, "H": C * P, "SW": Z0 + 16 + W + PB, "hb": 176, "keep": NL,
                     "u2": 2 * LC, "u1": 2 * LC, "vals": PB, "nl": 16, "rows": 512, "ones": 896, "MB": 896, "ME": 528,
                     "IDN": 128, "LS": 144, "L2": 144, "L8": 144, "NW": 144, "PN": 1024, "BO": 128, "SC": 128,
                     "tmp": 896, "base": 512, "QM": 2048, "MX": 1152, "crow": PB})):
    for _k, _n in _l.items():
        SCRATCH[_k] = ("sbuf", [128, _n], _d)
for _b in range(8):
    SCRATCH["ps%d" % _b] = ("psum", [128, 512], F32)

SEMAPHORES = (["pe", "dve", "act", "pool", "sent", "aux", "aud"] + ["sx%d" % i for i in range(N)]
              + ["ex%d" % i for i in range(N)] + ["el%d" % i for i in range(N)] + ["dm%d" % i for i in range(60)])

CFG = {"parts": ((0, 768), (768, 1280)), "chunks": ((0, 768), (768, 1280)), "xfirst": True, "dmafill": ("WN", "TT1"),
       "cuts": (0, 320, 640, 960, 1280, 1920, 2560, 3200, 3840),
       "ks": ((0, 1), (1, 2), (2, 3)),
       "seed": 4, "early": -1.0, "iters": 60000, "soon": 0.1, "temp": 0.0015,
       "mix": (0.25, 0.5, 0.7, 0.5), "period": 11.0}
STAGES = {"tot": (-7.2, -6.1), "h": (-6.65, -5.7), "H": (-6.45, -5.55), "Hs": (-6.15, -5.3), "u2": (-6.0, -5.15),
          "Ix": (-6.7, -6.6, -5.9), "pen": (-5.8, -5.5, -5.0), "xm": (-5.45, -5.1, -4.6), "repWN": (-4.7, -4.1),
          "u16": (-4.7,), "u1": (-4.62,), "n": (-4.3,), "nl": (-3.65,), "vals": (-3.7, -3.0), "D2": (-3.4,), "Z": (-3.1,),
          "U": (-3.0,), "so": (-2.75,), "so16": (-2.6,), "scat": (-2.45,), "Ts": (-1.3,), "repTT0": (-0.6,),
          "repTT1": (-0.6,), "": (-0.6,), "xd": (-5.8, -4.95), "ji": (-1.0,), "j16": (1.95,),
          "gat": (0.0, 0.0, 1.15, 1.15, 2.3, 3.0), "xs": (2.3, 3.85), "F": (2.0, 3.05, 8.2), "keep": (3.8, 3.95, 9.0),
          "tg": (3.85, 4.5, 4.9, 6.4, 6.9, 6.95, 8.0, 9.0), "Nb": (4.1, 9.1, 9.2), "N": (7.0, 8.9, 10.1),
          "Lb": (7.95, 9.7, 10.9), "L": (8.1, 10.0, 11.1), "o16": (9.75, 10.4, 11.3)}
QUEUES = {"h": "aa", "u2": "dd", "xm": "aad", "u1": "d", "nl": "a", "vals": "-a", "xd": "dd", "ji": "a", "gat": "daadaa",
          "keep": "aaa", "tg": "aaaaadaa"}
BASE = {"cyc": 0.9e-3, "pe": 0.5e-3, "mm": 0.004, "fix": 0.055, "lat": 0.07, "gat": 1.55, "sca": 3.8, "dma": 1.2,
        "bw": 500e3, "row": 0.015, "hold": 0.06, "call": 0.5, "first": 1.2, "rem": 1.2, "xbw": 80e3}
MODELS = [{}, {"cyc": 1.15e-3, "pe": 0.6e-3, "gat": 1.9, "sca": 2.5, "dma": 1.0, "bw": 600e3, "row": 0.01},
          {"cyc": 0.85e-3, "pe": 0.45e-3, "gat": 1.15, "sca": 5.0, "dma": 1.5, "bw": 420e3, "row": 0.02, "first": 2.0, "lat": 0.1}]
STATS = {}


def relays(T, topo, src, dst):
    if topo.may_write(src, dst):
        return None
    can = [c for c in topo.cores_of(src) if c != src and T.rank_of(c) is None and topo.may_write(c, dst)]
    same = topo.host(src) == topo.host(dst)
    pick = [c for c in can if (topo.die(c) == topo.die(src)) == same]
    return (pick or can)[0]


def emask(es):
    m = 0
    for e in es:
        m |= 1 << e
    return m


def relay_program(g, core, T, topo, s, d):
    dst = T.cores[d]
    rid, pid = topo.addr(dst, core)
    es = topo.engines(core, dst)
    n = len(topo.engines(T.cores[s], core))
    xs = slice(PB * s, PB * s + PB)
    home = [(T.sem["ex%d" % s], n // 2, T.XE[:, xs]), (T.sem["el%d" % s], n // 2, T.LE[:, NL * s:NL * s + NL])]
    jobs = [(T.sem.aux, n // 4, T.AL[s]), (T.sem["sx%d" % s], n // 2, T.XL[:, xs]), (T.sem.aud, n // 4, T.DL[s])]
    jobs += home if CFG["xfirst"] else home[::-1]
    for sem, cnt, ap in jobs:
        g.wait_ge(sem, cnt)
        g.remote_dma(ap, ap, sem, T.sem.sent, pid, rid, emask(es))
    g.wait_ge(T.sem.sent, len(jobs) * len(es))


def rank_program(g, core, T, topo):
    me = T.rank_of(core)
    if me is None:
        for s in range(N):
            for d in range(N):
                if s != d and relays(T, topo, T.cores[s], T.cores[d]) == core:
                    relay_program(g, core, T, topo, s, d)
        return
    cf = CFG
    Q = {"pe": g.tensor, "dve": g.vector, "act": g.scalar, "pool": g, "sp": g.sync}
    ops = []
    hist = {}
    mcache = {}

    def A(name, lo=0, hi=None, step=1, part=(0, 128)):
        hi = SCRATCH[name][1][-1] if hi is None else hi
        key = (lo, hi, step)
        if key not in mcache:
            mcache[key] = ((1 << (hi - lo)) - 1) << lo if step == 1 else emask(range(lo, hi, step))
        ap = T[name][part[0]:part[1], lo:hi] if step == 1 else T[name][part[0]:part[1], lo:hi:step]
        return {"ap": ap, "buf": name, "mask": mcache[key], "n": len(range(lo, hi, step)), "dt": SCRATCH[name][2]}

    def slot(name, mask):
        return {"buf": name, "mask": mask}

    today = []

    def add(var, rd, wr, sem=None, after=(), behind=(), name=""):
        i = len(ops)
        pre = {}
        for o, w in [(o, False) for o in rd] + [(o, True) for o in wr]:
            ps = o["buf"].startswith("ps")
            mk = 1 if ps else o["mask"]
            lst = hist.setdefault(o["buf"], [])
            for (j, m2, w2) in lst:
                if j != i and m2 & mk and (ps or w or w2):
                    pre[j] = pre.get(j, False) or not ps
            if w or ps:
                lst[:] = [e for e in lst if e[1] & ~mk or e[0] == i]
            lst.append((i, mk, w))
        for j in after:
            pre[j] = True
        for j in behind:
            pre[j] = pre.get(j, False)
        kind = ("", i)
        if today:
            kind = (name, today.count(name))
            today.append(name)
        ops.append({"var": var, "pre": pre, "sem": sem, "name": name, "kind": kind, "day": today[0] if today else None})
        return i

    def cyc(n, k=1.0):
        return {"fix": 1, "cyc": max(n * k, 64)}

    def narrow(*os_):
        return 0.5 if all(o["dt"] in (BF, U16) for o in os_) else 1.0

    def sc(x):
        return x["ap"] if isinstance(x, dict) else x

    def scs(*xs):
        return [x for x in xs if isinstance(x, dict)]

    def activation(out, in0, func, bias, scale):
        return cyc(out["n"]), lambda q: q.activation(out["ap"], in0["ap"], func, bias=sc(bias), scale=sc(scale))

    def ts(out, in0, s1, s2, op0, op1=None, act=None, name=""):
        def f(q):
            if op1 is None:
                return q.tensor_scalar(out["ap"], in0["ap"], sc(s1), None, op0)
            return q.tensor_scalar(out["ap"], in0["ap"], sc(s1), sc(s2), op0, op1)
        var = {"dve": (cyc(out["n"], narrow(out, in0)), f)}
        if act is not None:
            var["act"] = activation(out, in0, *act)
        return add(var, [in0] + scs(s1, s2) + scs(*(act or ())), [out], name=name)

    def scale(out, in_, s, b=0.0, name=""):
        return ts(out, in_, s, b, ALU.mult, ALU.add, act=(ACTF.Identity, b, s), name=name)

    def sign(out, in_, lo=-1.0, hi=1.0, name=""):
        return ts(out, in_, lo, hi, ALU.max, ALU.min, act=(ACTF.Sign, 0.0, hi), name=name)

    def cp(out, in0, both=True, name=""):
        var = {"dve": (cyc(out["n"], narrow(out, in0)), lambda q: q.tensor_copy(out["ap"], in0["ap"]))}
        if both:
            var["act"] = (cyc(out["n"]), lambda q: q.activation(out["ap"], in0["ap"], ACTF.Copy))
        return add(var, [in0], [out], name=name)

    def tt(out, a, b, op, name=""):
        k = 1.0 if (a["buf"].startswith("ps") or b["buf"].startswith("ps")) else 2.0
        return add({"dve": (cyc(out["n"], k), lambda q: q.tensor_tensor(out["ap"], a["ap"], b["ap"], op))}, [a, b], [out], name=name)

    def ms(out, v):
        return add({"dve": (cyc(out["n"], narrow(out)), lambda q: q.memset(out["ap"], v))}, [], [out])

    def scan(out, d0, d1, init, op0, op1, name=""):
        return add({"dve": (cyc(out["n"], narrow(out, d0, d1)), lambda q: q.tensor_tensor_scan(
            out["ap"], d0["ap"], d1["ap"], sc(init), op0, op1))}, [d0, d1] + scs(init), [out], name=name)

    def mm(items, name="", start=True, stop=True):
        t = sum(max(64, o["n"]) * (4 if r["dt"] == F32 else 1) for o, l, r in items)

        def f(q):
            ins = None
            for i, (o, l, r) in enumerate(items):
                ins = q.matmul(o["ap"], l["ap"], r["ap"], start and i == 0, stop and i == len(items) - 1)
            return ins
        return add({"pe": ({"pe": t, "mm": len(items), "tail": 0.05}, f)}, [x for o, l, r in items for x in (l, r)],
                   [items[0][0]], name=name)

    def iota_call(out, pattern, base, cm):
        t = {"us": 0.13, "cyc": 2 * out["n"]}
        if out["dt"] == I32:
            return t, lambda q: q.iota(out["ap"], pattern, base, cm)
        return t, lambda q: q.iota(out["ap"], pattern, base, cm, allow_small_or_imprecise_dtypes=True)

    def iota(out, pattern, base, cm):
        return add({"pool": iota_call(out, pattern, base, cm)}, [], [out])

    def asel(out, in_, pattern, base, cm):
        return add({"pool": ({"us": 0.17, "cyc": 2 * out["n"]}, lambda q: q.affine_select(
            out["ap"], in_["ap"], pattern, ALU.is_equal, 0.0, base, cm))}, [in_], [out])

    ndma = [0]

    def dmas(jobs, rd, wr, nbytes, rows, qs=("sp", "act"), after=(), name=""):
        sem = T.sem["dm%d" % ndma[0]]
        ndma[0] += 1

        def f(q):
            for o, i in jobs:
                q.dma_start(o, i).then_inc(sem, 16)
        cost = {"hold": len(jobs), "bytes": nbytes, "rows": rows, "dma": 1}
        return add({e: (cost, f) for e in qs}, rd, wr, sem=(sem, 16 * len(jobs)), after=after, name=name)

    def arrive(sem, cnt, wr, after, hops, nbytes):
        return add({"ext": ({"hops": hops, "far": nbytes}, None)}, [], wr, sem=(sem, cnt), after=after)

    others = [d for d in range(N) if d != me]
    via = {d: relays(T, topo, core, T.cores[d]) for d in others}
    hop = {d: (via[d] if via[d] is not None else T.cores[d]) for d in others}
    far = sorted([d for d in others if via[d] is not None], key=lambda d: topo.die(via[d]) == topo.die(core))
    near = [d for d in others if via[d] is None]
    sent = [0]
    calls = []

    def xfer(d, es, src, dst, sem):
        rid, pid = topo.addr(hop[d], core)
        sent[0] += len(es)
        return RemoteDMATransfer(dst_ids=[DstId(rid=rid, pnc=pid)], dma_engine_mask=emask(es), remote_sem=sem, src=src, dst=dst)

    def send(trs, rd, nbytes):
        cost = {"call": 1, "first": 0 if calls else 1, "bytes": nbytes * len(trs), "rows": 128 * len(trs), "rem": 1}
        calls.append(add({"pool": (cost, lambda q: q.remote_dma_fused(trs, local_sem=T.sem.sent))}, rd, [], sem="none",
                         behind=calls[-1:], name="send"))
        return calls[-1]

    def send_s(src, to, sem, nbytes):
        e, d = topo.engines(core, hop[far[0]]), near[0]
        a = send([xfer(f, e[i::2], src(f)["ap"], to, sem) for i, f in enumerate(far)], [src(f) for f in far], nbytes)
        b = send([xfer(d, topo.engines(core, hop[d]), src(d)["ap"], to, sem)], [src(d)], nbytes)
        return a, b

    def send_d(src, land, sem, nbytes):
        d = near[0]
        e0 = topo.engines(core, hop[d])
        e = [x for x in topo.engines(core, hop[far[0]]) if x not in e0]
        trs = [xfer(f, e[i::2], T[src][f], T[land][me], sem) for i, f in enumerate(far)]
        return send(trs + [xfer(d, e0, T[src][d], T[land][me], sem)], [slot(src, 15)], nbytes)

    def got(s):
        r = relays(T, topo, T.cores[s], core)
        return len(topo.engines(r if r is not None else T.cores[s], core))

    def piece(name):
        return lambda d: A(name, PB * d, PB * d + PB)

    dmas([(T.AO[:, 0:96, :], T.nb[:]), (T.AO[:, 96:128, :], T.res[:])], [], [slot("AO", 1)], 163840, 32, name="ldl")
    for d in far + near + [me]:
        blk = A("XI", PB * d, PB * d + PB)
        dmas([(blk["ap"], T.x0[32 * d:32 * d + 32, :])], [], [blk], 128 * PB * 4, 128, name="ldx")
        cp(A("XL" if d == me else "XO", PB * d, PB * d + PB), blk, both=False, name="cvx")
    dmas([(T.DO[:], T.dice[:])], [], [slot("DO", 1)], 122880, 16, name="ldd")
    sl = send_d("AO", "AL", T.sem.aux, 40960)
    sa, sb = send_s(piece("XO"), T.XL[:, PB * me:PB * me + PB], T.sem["sx%d" % me], 81920)
    sd = send_d("DO", "DL", T.sem.aud, 30720)
    left = arrive(T.sem.sent, sent[0], [], [sl, sa, sb, sd], 0, 0)
    dmas([(T.AL[me], T.AO[me])], [slot("AO", 1)], [slot("AL", 1)], 40960, 16)
    dmas([(T.DL[me], T.DO[me])], [slot("DO", 1)], [slot("DL", 1)], 30720, 16)
    arrive(T.sem.aux, sum(got(s) for s in others), [slot("AL", 2)], [sl], 2.5, 40960)
    for s in near + far:
        arrive(T.sem["sx%d" % s], got(s), [A("XL", PB * s, PB * s + PB)], [sb if s in near else sa], 0.5 if s in near else 2, 81920)
    arrive(T.sem.aud, sum(got(s) for s in others), [slot("DL", 2)], [sd], 2, 30720)
    dmas([(T.LI[:], T.AL[:, 0:96, :])], [slot("AL", 3)], [A("LI")], 122880, 128)
    dmas([(T.RI[:], T.AL[:, 96:128, :])], [slot("AL", 3)], [A("RI")], 40960, 128)
    dmas([(T.DI[:], T.DL[:])], [slot("DL", 3)], [A("DI")], 122880, 128)

    def mat(name, i):
        return A(name, 128 * i, 128 * i + 128)

    def col(name, i):
        return A(name, i, i + 1)

    ms(A("ones"), 1.0)
    ms(A("zf"), 8.0)
    ms(A("z0"), 0.0)
    add({"act": ({"fix": 1, "cyc": 64, "us": 1.3}, lambda q: q.activation(T.hb[:, 0:1], T.ones[:, 0:1], ACTF.Tanh, scale=-16.0))},
        [col("ones", 0)], [col("hb", 0)])
    iota(col("pi", 0), [[0, 1]], 0, 1)
    asel(A("IDN"), A("ones", 0, 128), [[1, 128]], 0, -1)
    asel(A("MB"), A("ones"), [[1, 4], [4, 224]], -384, -1)
    asel(A("ME"), A("ones", 0, 528), [[1, 528]], -3, -4)
    iota(mat("rows", 0), [[0, 8], [1, 16]], 0, 0)
    iota(mat("rows", 1), [[1, 8], [0, 16]], 0, 0)
    iota(mat("rows", 2), [[0, 4], [1, 2], [0, 16]], 0, 0)
    iota(mat("rows", 3), [[16, 8], [0, 2], [1, 8]], 0, 0)
    iota(A("r16"), [[1, 144]], 0, 0)
    iota(A("crow"), [[1, PB]], -VOFF, 0)
    p = col("pi", 0)
    ts(col("pb", 0), p, 15, None, ALU.bitwise_and)
    ts(col("pb", 1), p, 4, None, ALU.logical_shift_right)
    ts(col("pb", 2), p, 4, 1, ALU.logical_shift_right, ALU.bitwise_and)
    ts(col("pb", 3), p, 5, None, ALU.logical_shift_right)
    ts(col("pb", 4), p, 7, None, ALU.bitwise_and)
    cp(A("pf", 0, 5), A("pb", 0, 5), both=False)
    cp(col("pf", 5), p, both=False)
    p16, pg, pc, pq, p8 = [col("pf", i) for i in range(5)]
    ts(A("cols", 0, 8), A("r16", 0, 8), p8, -64.0, ALU.is_equal, ALU.mult)
    ts(col("cols", 12), p16, 8.0, None, ALU.is_lt)
    ts(col("cols", 13), p16, 8.0, None, ALU.is_ge)
    ts(col("cols", 14), p16, 15.0, None, ALU.is_equal)
    e15 = col("cols", 14)
    wgt, tsc, step, own, row15, p21, zone0, jbase, cmul = [col("cols", 15 + i) for i in range(9)]
    for out, src, a, b in ((wgt, e15, -16.0 * M - 0.5, 0.5),
                           (tsc, e15, -15, 16),
                           (step, e15, -1.0 / 128, 1.0 / 128), (own, pq, -P, Z0), (row15, pg, 16, 15), (p21, p16, -1, -W),
                           (zone0, pq, -P, Z0 + 16), (jbase, pq, P, ROUND - Z0 - W // 2), (cmul, e15, 1.0 / M, 0)):
        scale(out, src, float(a), float(b))
    ts(col("cols", 24), e15, -15.0, p16, ALU.mult, ALU.add)
    scale(A("crow"), A("crow"), cmul, col("cols", 24))
    IDN = A("IDN")
    ts(A("LS"), A("r16"), row15, None, ALU.is_equal)
    scale(A("NW"), A("LS"), wgt)
    scale(A("L2"), A("LS"), 2.0)
    ts(A("BO"), mat("rows", 1), pg, None, ALU.is_equal)
    ts(A("SC"), mat("rows", 2), pc, None, ALU.is_equal)
    for r in range(8):
        scale(mat("PN", r), A("BO"), col("cols", r))
    ts(mat("tmp", 0), mat("rows", 0), p16, None, ALU.is_gt)
    ts(mat("tmp", 1), mat("rows", 0), p16, None, ALU.is_le)
    ts(mat("tmp", 2), mat("rows", 0), p16, None, ALU.is_ge)
    ts(mat("tmp", 3), mat("rows", 0), p16, -8192.0, ALU.is_equal, ALU.mult)
    ts(mat("tmp", 4), mat("rows", 0), 15.0, None, ALU.is_lt)
    E8, I4096, ZERO, HA, HU, TB, NB = [mat("MX", i) for i in range(7)]
    half = [mat("MX", 7), mat("MX", 8)]
    for e in range(2):
        scale(half[e], IDN, col("cols", 12 + e))
    pk = col("pf", 5)
    ts(E8, mat("rows", 3), pk, 1024.0, ALU.is_equal, ALU.mult)
    ts(mat("tmp", 5), mat("rows", 3), pk, None, ALU.is_gt)
    ts(mat("tmp", 6), mat("rows", 3), pk, col("cols", 12), ALU.is_le, ALU.mult)
    tt(A("L8", 8, 144), A("L2", 8, 144), A("L2", 0, 136), ALU.add)
    scale(I4096, IDN, 4096.0)
    scale(ZERO, IDN, 0.0)
    scale(TB, IDN, 1.0, -2.0 * TH / 128)
    scale(NB, IDN, -7.5, -16.0 * VOFF / 128)
    scale(A("NI"), IDN, -1.0)
    tt(mat("tmp", 5), mat("tmp", 5), A("BO"), ALU.mult)
    tt(HA, mat("tmp", 5), E8, ALU.subtract)
    tt(HU, mat("tmp", 6), A("BO"), ALU.mult)
    tt(mat("tmp", 2), mat("tmp", 2), mat("tmp", 4), ALU.mult)
    for b in range(4):
        tt(mat("base", b), mat("tmp", b), A("SC"), ALU.mult)
    ts(A("cols", 8, 12), A("r16", 0, 4), pq, None, ALU.is_equal)
    for q in range(N):
        scale(A("QM", 512 * q, 512 * q + 512), A("base"), col("cols", 8 + q))

    def ofrank(q, b, src):
        return mat("QM", 4 * q + b), A(*src)

    ts(A("NK", 0, 20), A("r16", 0, 20), -16.0, p21, ALU.mult, ALU.add)
    zone = A("SW", Z0, Z0 + P + 16)
    ms(zone, -256.0)
    scale(A("DT"), zone, step)

    def fill(out, v, part=(0, 128), wr=None, qs=("dve", "act", "pool")):
        src = A("DT", 0, out["n"], part=part)
        var = {"dve": (cyc(out["n"], 0.5), lambda q: q.memset(out["ap"], float(v))),
               "act": activation(out, src, ACTF.Identity, float(v), 0.0), "pool": iota_call(out, [[0, out["n"]]], v, 0)}
        return add({e: var[e] for e in qs}, [src] if "act" in qs else [], [wr or out], name="fill")

    spare = {}
    for name in ("WN", "TT0", "TT1"):
        spare[name] = slot(name + "x", 127)
        parts = [(0, 32 * (N - 1 - b)) if b < N - 1 else (32 * (2 * N - 1 - b), 128) for b in range(2 * N - 1)]
        if name in cf["dmafill"]:
            dmas([(T[name][a:z, P * b:P * b + P], T.DT[a:z, 0:P]) for b, (a, z) in enumerate(parts) if b != N - 1],
                 [A("DT")], [spare[name], A(name, Z0 - 16, Z0)], 983040, 384, qs=("sp",), after=[left], name="dfill")
            continue
        for b, part in enumerate(parts):
            qs = ("pool",)
            if b in (N - 2, 2 * N - 2):
                fill(A(name, P * b, P * b + P), 0, qs=qs)
            elif b != N - 1:
                fill(A(name, P * b, P * b + P, part=part), 0, part, slot(name + "x", 1 << b), qs)
    for k, v in enumerate((-1024, 0, 0)):
        fill(A("D0", k, 4 * P, 4), v, qs=("dve", "act"))

    def spread(name, c0, c1):
        jobs, wr = [], []
        for s in range(1, N):
            cut = 128 - 32 * s
            a, b = Z0 + P * s, Z0 + P * (s - N)
            jobs += [(T[name][0:cut, a + c0:a + c1], T[name][32 * s:128, Z0 + c0:Z0 + c1]),
                     (T[name][cut:128, b + c0:b + c1], T[name][0:32 * s, Z0 + c0:Z0 + c1])]
            wr += [A(name, a + c0, a + c1), A(name, b + c0, b + c1)]
        dmas(jobs, [A(name, Z0 + c0, Z0 + c1)], wr, (N - 1) * 256 * (c1 - c0), (N - 1) * 128, qs=("sp",), name="rep" + name)

    def LSr(name, r):
        return A(name, 15 - r, 143 - r)

    def X(lo, hi, step=1):
        return A("S", 4 * lo + 3, 4 * hi, 4 * step)

    def ps(b, lo, hi, step=1):
        return A("ps%d" % b, lo, hi, step)

    for i, q in enumerate([me] + near + far):
        for b in range(4):
            mm([(ps(b, 0, PB), A("MB", 224 * b + 96 - 32 * q, 224 * b + 224 - 32 * q), A("XL", PB * q, PB * q + PB))], "place", i == 0, i == N - 1)
    for b in range(4):
        cp(X(PB * b, PB * b + PB), ps(b, 0, PB), name="x0")
    for e in range(2):
        ts(A("R2", LC * e, LC * e + LC), A("RI"), col("cols", 12 + e), None, ALU.mult)
    for j, (b0, b1) in enumerate(((0, 6), (6, 12), (12, 16))):
        for b in range(b0, b1):
            mm([(ps(5 + j, LC * (b - b0), LC * (b - b0 + 1)), mat("PN", b % 8), A("R2", LC * (b // 8), LC * (b // 8 + 1)))])
        scale(A("D0", 4 * LC * b0 + 3, 4 * LC * b1, 4), ps(5 + j, 0, LC * (b1 - b0)), 1.0 / 64, name="res")
    cp(A("L"), A("LI"), both=False)
    ts(A("o16"), A("LI"), own, None, ALU.add, name="o16")
    for t in range(DAYS):
        src = A("DI")
        if t:
            ts(A("da"), src, float(STEP * t), None, ALU.add, name="da")
            src = A("db")
            ts(src, A("da"), M - 1, None, ALU.bitwise_and, name="db")
        ts(A("DD", NL * t, NL * t + NL), src, 1.0 / M, None, ALU.mult, name="dd")
    bank = [0]

    def nextbank():
        bank[0] += 1
        return (bank[0] - 1) % 3

    for t in range(DAYS):
        today[:] = [t]
        tn, un = "TT%d" % (t % 2), LC * (t % 2)
        for pi_, (p0, p1) in enumerate(cf["parts"]):
            c0, c1, pb = p0 // 8, p1 // 8, 3 + pi_ % 2
            o = ps(pb, c0, c1)
            mm([(o, TB, A("ones", c0, c1))] + [(o, LSr("L8", r), X(p0 + r, p1, 8)) for r in range(8)], "tot")
            sign(A("hb", c0 + 1, c1 + 1), o, name="h")
            o = ps(pb, 2 * LC + c0, 2 * LC + c1)
            mm([(o, HA, A("hb", c0 + 1, c1 + 1)), (o, HU, A("hb", c0, c1)), (o, E8, A("hb", c0, c1))], "H")
            scan(A("hs", c0, c1), o, A("zf", c0, c1), col("hs", c0 - 1) if c0 else float(2 * (1024 - CAP) + 1), ALU.add, ALU.add, name="Hs")
            sign(A("u2", c0, c1), A("hs", c0, c1), name="u2")
            k = -(-(p1 - p0) // 512)
            n = (p1 - p0) // k
            mine = [(nextbank(), p0 + n * i) for i in range(k)]
            for b, lo in mine:
                mm([(ps(b, 0, n), IDN, X(lo, lo + n))], "Ix", True, False)
            for b, lo in mine:
                mm([(ps(b, r, n, 8), mat("PN", r), A("u2", lo // 8, (lo + n) // 8)) for r in range(8)], "pen", False, True)
                scale(A("WN", Z0 + lo, Z0 + lo + n), ps(b, 0, n), 1.0, -128.0, name="xm")
            spread("WN", p0, p1)
        u1 = A("u1", un, un + LC)
        mm([(ps(5, PB, PB + LC), half[e], A("u2", e, 2 * LC, 2)) for e in range(2)], "u16")
        cp(u1, ps(5, PB, PB + LC), name="u1")
        for p0, p1 in cf["chunks"]:
            ts(A("G", 4 * p0 + 3, 4 * p1, 4), X(p0, p1), float(-DEC), 0.0, ALU.add, ALU.max,
               act=(ACTF.Relu, float(-DEC), 1.0), name="xd")
        mm([(ps(3, 352, 357), LSr("LS", r), A("u1", un + r, un + LC, 16)) for r in range(16)], "n")
        nl = A("nl", 0, 5)
        scale(nl, ps(3, 352, 357), 0.5, 8.0, name="nl")
        mm([(ps(3, 384, 405), ZERO, A("ones", 0, 21))]
           + [(ps(3, 384 + 5 * q, 389 + 5 * q),) + ofrank(q, 0, ("nl", 0, 5)) for q in range(N)]
           + [(ps(3, 385 + 5 * q, 390 + 5 * q),) + ofrank(q, 1, ("nl", 0, 5)) for q in range(N)], "D2")
        mm([(ps(4, 352, 372), A("NI"), A("NK", 0, 20))]
           + [(ps(4, 352 + 5 * q, 357 + 5 * q),) + ofrank(q, 3, ("nl", 0, 5)) for q in range(N)], "Z")
        scan(A("U", 0, 21), ps(3, 384, 405), A("z0", 0, 21), 0.0, ALU.add, ALU.add, name="U")
        tt(A("so", 0, 20), A("U", 0, 20), ps(4, 352, 372), ALU.max, name="so")
        sw, so16, vals = A("SW"), A("so16", 0, 20), A("vals")
        ts(so16, A("so", 0, 20), zone0, None, ALU.add, name="so16")
        mm([(ps(5, 0, PB), IDN, A("crow"))]
           + [(ps(5, LC * q, LC * (q + 1)),) + ofrank(q, 2, ("u1", un, un + LC)) for q in range(N)], "vals")
        cp(vals, ps(5, 0, PB), name="vals")
        add({"dve": ({"fix": 1, "sca": PB}, lambda q: q.tensor_copy(sw["ap"].indirect(so16["ap"]), vals["ap"]))},
            [so16, vals], [sw], name="scat")
        scan(A(tn, Z0 - 16, Z0 + P), A("DT"), zone, -256.0, ALU.add, ALU.max, name="Ts")
        spread(tn, 0, P)
        if t < DAYS - 1:
            iota(zone, [[0, P + 16]], -256, 0)
        scale(A("ji"), A("DD", NL * t, NL * t + NL), col("U", 20), -(W / 2 + 0.5 - 0.5 / M), name="ji")
        ts(A("j16", NL * (t % 2), NL * (t % 2 + 1)), A("ji"), ROUND, jbase, ALU.add, ALU.subtract, name="j16")
        win = A("WN")
        for p0, p1 in cf["chunks"]:
            cost = {"fix": 1, "gat": p1 - p0}
            for k in range(C):
                o = A("G", 4 * p0 + k, 4 * p1, 4)
                off = A("o16", LC * k + p0 // 16, LC * k + p1 // 16)
                add({"dve": (cost, lambda q, o=o, off=off: q.tensor_copy(o["ap"], win["ap"].indirect(off["ap"]))),
                     "act": (cost, lambda q, o=o, off=off: q.activation(o["ap"], win["ap"].indirect(off["ap"]), ACTF.Copy))},
                    [win, spare["WN"], off], [o], name="gat")
            scan(A("S", 4 * p0, 4 * p1), A("D0", 4 * p0, 4 * p1), A("G", 4 * p0, 4 * p1), 0.0, ALU.add, ALU.max, name="xs")
        for h0, h1 in zip(cf["cuts"], cf["cuts"][1:]):
            o, tab, cost = A("H", h0, h1), A(tn), {"fix": 1, "gat": h1 - h0}
            off = A("j16", NL * (t % 2) + h0 // 16, NL * (t % 2) + h1 // 16)
            got_ = tab["ap"].indirect(off["ap"])
            add({"act": (cost, lambda q, o=o, x=got_: q.activation(o["ap"], x, ACTF.Tanh, scale=tsc["ap"])),
                 "dve": (cost, lambda q, o=o, x=got_: q.tensor_scalar(o["ap"], x, -1.0, 1.0, ALU.max, ALU.min))},
                [tab, spare[tn], off, tsc], [o], name="tg")
        for i, (k0, k1) in enumerate(cf["ks"]):
            for k in range(k0, k1):
                o = ps(6 + min(i, 1), LC * k, LC * k + LC)
                mm([(o, I4096, u1)] + [(o, LSr("L2", r), A("G", 4 * r + k, 4 * P, 64)) for r in range(16)], "F")
            ts(A("keep", LC * k0, LC * k1), ps(6 + min(i, 1), LC * k0, LC * k1), 5500.0, 16384.0, ALU.is_lt, ALU.mult,
               act=(ACTF.Relu, 44000.0, -8.0), name="keep")
        for i, (k0, k1) in enumerate(cf["ks"]):
            a, b, pb = LC * k0, LC * k1, 6 + i % 2
            mm([(ps(pb, NL + a, NL + b), NB, A("ones", a, b)), (ps(pb, NL + a, NL + b), IDN, A("keep", a, b))], "Nb", True, False)
            for k in range(k0, k1):
                mm([(ps(pb, NL + LC * k, NL + LC * k + LC), LSr("NW", r), A("H", P * k + r, P * k + P, 16)) for r in range(16)],
                   "N", False, k == k1 - 1)
            tt(A("Lb", a, b), ps(pb, NL + a, NL + b), A("L", a, b), ALU.min, name="Lb")
            add({"act": activation(A("L", a, b), A("Lb", a, b), ACTF.Abs, 0.0, 1.0)}, [A("Lb", a, b)], [A("L", a, b)], name="L")
            if t < DAYS - 1:
                ts(A("o16", a, b), A("L", a, b), own, None, ALU.add, name="o16")

    today[:] = []
    for b, d in enumerate(far + near + [me]):
        for j in range(4):
            mm([(ps(b, 0, PB), A("ME", 128 * d - j + 3, 128 * d - j + 131), X(PB * j, PB * j + PB))], "back", j == 0, j == 3)
        cp(A("YF" if d == me else "XS", PB * d, PB * d + PB), ps(b, 0, PB), name="out")
    cp(A("LU"), A("L"), both=False, name="lu")
    home = [lambda: send_s(piece("XS"), T.XE[:, PB * me:PB * me + PB], T.sem["ex%d" % me], 81920),
            lambda: send_s(lambda d: A("LU"), T.LE[:, NL * me:NL * me + NL], T.sem["el%d" % me], 61440)]
    if cf["xfirst"]:
        sx, sl = home[0](), home[1]()
    else:
        sl, sx = home[1](), home[0]()
    rows = (32 * me, 32 * me + 32)
    dmas([(T.ynb[32 * me:32 * me + 32, :], T.L[32 * me:32 * me + 32, :])], [A("L")], [], 30720, 32)
    blk = A("YF", PB * me, PB * me + PB)
    dmas([(T.yx[32 * me:32 * me + 32, :], blk["ap"])], [blk], [], 163840, 128)
    for s in near + far:
        i, hops = (1, 0.5) if s in near else (0, 1.5)
        land, blk = A("XE", PB * s, PB * s + PB), A("YF", PB * s, PB * s + PB)
        arrive(T.sem["ex%d" % s], got(s), [land], [sx[i]], hops, 81920)
        cp(blk, land, name="cvy")
        dmas([(T.yx[32 * s:32 * s + 32, :], blk["ap"])], [blk], [], 163840, 128, name="stx")
        land, blk = A("LE", NL * s, NL * s + NL, part=rows), A("YL", NL * s, NL * s + NL, part=rows)
        arrive(T.sem["el%d" % s], got(s), [land], [sl[i]], hops, 61440)
        cp(blk, land, both=False, name="cvl")
        dmas([(T.ynb[32 * s:32 * s + 32, :], blk["ap"])], [blk], [], 30720, 32, name="stl")

    n = len(ops)
    pres = [[(j, w or ops[j]["sem"] not in (None, "none")) for j, w in o["pre"].items()] for o in ops]
    above = [0] * n
    for i in range(n):
        for j, w in pres[i]:
            above[i] |= above[j] | 1 << j
        pres[i] = [(j, w) for j, w in pres[i] if not any(above[k] >> j & 1 for k, _ in pres[i])]
    succ = [[] for _ in ops]
    for i in range(n):
        for j, w in pres[i]:
            succ[j].append((i, w))

    def order(key):
        return sorted(range(n), key=lambda i: (key[i], i))

    def times(c, m):
        x = lambda k: c.get(k, 0)
        hold = (x("fix") * m["fix"] + (x("cyc") + x("gat") * m["gat"] + x("sca") * m["sca"]) * m["cyc"] + x("pe") * m["pe"]
                + x("mm") * m["mm"] + x("us") + x("hold") * m["hold"] + x("call") * m["call"] + x("first") * m["first"])
        if "bytes" in c:
            wait = x("dma") * m["dma"] + x("rem") * m["rem"]
            return hold, x("first") * m["first"] + 0.6 * wait, x("bytes") / m["bw"] + x("rows") * m["row"] / 16, 0.4 * wait
        return hold, hold, 0.0, x("tail") + x("hops") * m["rem"] + x("far") / m["xbw"]

    tms = []
    for d in MODELS:
        m = dict(BASE, **d)
        tms.append((m["lat"], [{e: times(v[0], m) for e, v in o["var"].items()} for o in ops]))

    def place(line, lo, busy):
        k = len(line)
        while k and line[k - 1][1] > lo:
            k -= 1
        while k < len(line) and lo + busy > line[k][0] + 1e-9:
            lo = max(lo, line[k][1])
            k += 1
        return lo, k

    def forward(key, bias, model):
        lat, tm = tms[model]
        start, held, done, eng = [0.0] * n, [0.0] * n, [0.0] * n, [None] * n
        lines = {e: [] for e in list(Q) + ["dq"]}
        key = list(key)
        for i in range(n):
            for j, w in pres[i]:
                if key[j] > key[i]:
                    key[i] = key[j]
        for i in order(key):
            best = None
            for e, v in tm[i].items():
                lo, k = 0.0, 0
                for j, w in pres[i]:
                    x = done[j] if (w or eng[j] != e) else held[j]
                    if x > lo:
                        lo = x
                if e != "ext":
                    lo, k = place(lines[e], lo, v[0])
                f = lo + v[0] + (bias[i] if e == "dve" else 0.0)
                if best is None or f < best[0]:
                    best = (f, lo, e, k)
            _, lo, e, k = best
            v = tm[i][e]
            start[i], held[i], eng[i] = lo, lo + v[0], e
            if e != "ext":
                lines[e].insert(k, (lo, lo + v[0]))
            x = lo + v[1]
            if v[2]:
                x, k = place(lines["dq"], x, v[2])
                lines["dq"].insert(k, (x, x + v[2]))
            done[i] = x + v[2] + v[3] + lat
        return start, done, eng

    def replay(seq, eng, model, was=None, first=0):
        lat, tm = tms[model]
        free, last = dict.fromkeys(list(Q) + ["ext"], 0.0), dict.fromkeys(list(Q) + ["ext", "dq"])
        dq = 0.0
        if was is None:
            held, done, why = [0.0] * n, [0.0] * n, [None] * n
        else:
            held, done, why = was[2][:], was[3][:], was[4][:]
            for i in seq[first - 1::-1] if first else ():
                e = eng[i]
                if last[e] is None and e != "ext":
                    free[e], last[e] = held[i], i
                if last["dq"] is None and tm[i][e][2]:
                    dq, last["dq"] = done[i] - lat - tm[i][e][3], i
                if None not in (last["pe"], last["dve"], last["act"], last["pool"], last["sp"], last["dq"]):
                    break
        for i in seq[first:]:
            e = eng[i]
            lo, y = free[e], None
            for j, w in pres[i]:
                x = done[j] if (w or eng[j] != e) else held[j]
                if x >= lo:
                    lo, y = x, j
            v = tm[i][e]
            why[i] = (y, False) if y is not None else (last[e], True)
            held[i] = lo + v[0]
            if e != "ext":
                free[e], last[e] = held[i], i
            x = lo + v[1]
            if v[2]:
                if dq > x:
                    x, why[i] = dq, (last["dq"], True)
                x = dq = x + v[2]
                last["dq"] = i
            done[i] = x + v[3] + lat
        span = max(done)
        i, path = done.index(span), []
        while i is not None:
            j, queue = why[i]
            if queue and j is not None:
                path.append((j, i))
            i = j
        return span, path, held, done, why

    def shift(seq, i, j):
        a, b = seq.index(j), seq.index(i)
        if a > b or above[i] >> j & 1:
            return None
        mid = seq[a:b + 1]
        up = [x for x in mid if x == i or above[i] >> x & 1]
        return seq[:a] + up + [x for x in mid if not (x == i or above[i] >> x & 1)] + seq[b + 1:]

    def sink(seq, j, i):
        a, b = seq.index(j), seq.index(i)
        if a > b or above[i] >> j & 1:
            return None
        mid = seq[a:b + 1]
        down = [x for x in mid if x == j or above[x] >> j & 1]
        return seq[:a] + [x for x in mid if not (x == j or above[x] >> j & 1)] + down + seq[b + 1:]

    if "plan" not in STATS:
        rng = np.random.default_rng(cf["seed"])
        key, bias = [1e9] * n, [0.0] * n
        for i in range(n - 1, -1, -1):
            name, k = ops[i]["kind"]
            if ops[i]["day"] is not None:
                key[i] = cf["period"] * ops[i]["day"] + STAGES[name][k]
                bias[i] = {"a": 9.0, "d": -9.0, "-": 0.0}[QUEUES.get(name, "------")[k]]
            elif succ[i]:
                key[i] = min(key[j] for j, w in succ[i]) - min(sum(v[1:]) for v in tms[0][1][i].values())
                key[i] = min(key[i], cf["early"]) if ops[i]["name"] in ("da", "db", "dd", "fill") else key[i]
            else:
                key[i] = cf["period"] * (DAYS + 1)
        start, done, eng = forward(key, bias, 0)
        seq = order(start)
        twin = {(o["kind"], o["day"]): i for i, o in enumerate(ops)}
        best = cur = unit = None
        for it in range(cf["iters"]):
            if seq is not None:
                first = 0
                while cur and first < n and seq[first] == cur[1][first] and eng[seq[first]] == cur[2][seq[first]]:
                    first += 1
                runs = [replay(seq, eng, m, cur and cur[5][m], first) for m in range(len(tms))]
                unit = unit or [r[0] for r in runs]
                score = sum((r[0] + cf["soon"] * sum(r[3]) / n) / u for r, u in zip(runs, unit)) / len(unit)
                if best is None or score <= best[0]:
                    best = (score, seq, eng, [r[0] for r in runs])
                if cur is None or score <= cur[0] - cf["temp"] * (1 - it / cf["iters"]) * float(np.log(rng.random())):
                    cur = (score, seq, eng, [x for r in runs for x in r[1]], runs[0][2], runs)
            seq, eng, how = cur[1], cur[2], float(rng.random())
            j, i = cur[3][int(rng.integers(len(cur[3])))]
            if it % 50 == 0:
                seq = order([cur[4][x] - tms[0][1][x][eng[x]][0] for x in range(n)])
                continue
            if how >= cf["mix"][2]:
                x = int(rng.integers(n))
                line = [y for y in seq if eng[y] == eng[x]]
                k = line.index(x)
                y = min(max(k + int(rng.integers(-5, 6)), 0), len(line) - 1)
                j, i, how = (line[y], x, 0.0) if y < k else (x, line[y], cf["mix"][0])
            pairs = [(j, i)]
            if rng.random() < cf["mix"][3] and ops[j]["day"] is not None and ops[i]["day"] is not None:
                pairs = [(twin.get((ops[j]["kind"], ops[j]["day"] + d)), twin.get((ops[i]["kind"], ops[i]["day"] + d)))
                         for d in range(1 - DAYS, DAYS)]
                pairs = [x for x in pairs if None not in x]
            if how < cf["mix"][1]:
                for j, i in pairs:
                    seq = (shift(seq, i, j) if how < cf["mix"][0] else sink(seq, j, i)) or seq
                seq = None if seq is cur[1] else seq
            else:
                side = int(rng.integers(2))
                x = (j, i)[side]
                can = [e for e in ops[x]["var"] if e != eng[x]]
                if can:
                    eng, e = list(eng), can[int(rng.integers(len(can)))]
                    for y in pairs:
                        eng[y[side]] = e
                else:
                    seq = None
        STATS["plan"] = best
    seq, eng = STATS["plan"][1:3]
    span, path, held, done, why = replay(seq, eng, 0)
    STATS[me] = (span, [(held[i] - tms[0][1][i][eng[i]][0], done[i], eng[i], ops[i]["name"]) for i in seq])

    def needs(i):
        return [j for j, w in ops[i]["pre"].items() if ops[j]["sem"] != "none" and (eng[j] != eng[i] or w or ops[j]["sem"] is not None)]

    mine = [i for i in seq if eng[i] == "pool" and ops[i]["sem"] is None]
    for a, b in zip(mine, mine[1:]):
        if "fill" in (ops[a]["name"], ops[b]["name"]):
            ops[b]["pre"][a] = True
    pos = {}
    seen = {e: {} for e in Q}
    wanted = set()
    for i in seq:
        pos[i] = len(pos)
        if eng[i] == "ext":
            continue
        lastof = {}
        for j in needs(i):
            if ops[j]["sem"] is None and pos[j] > lastof.get(eng[j], (-1, -1))[0]:
                lastof[eng[j]] = (pos[j], j)
        for e, (pj, j) in lastof.items():
            if pj > seen[eng[i]].get(e, -1):
                seen[eng[i]][e] = pj
                wanted.add(j)
    count = {e: 0 for e in Q}
    val = {}
    seen = {e: {} for e in Q}
    waited = set()
    for i in seq:
        e = eng[i]
        if e == "ext":
            continue
        q = Q[e]
        top = {}
        for j in needs(i):
            if ops[j]["sem"] is not None:
                if seen[e].get(j) is None:
                    seen[e][j] = 1
                    waited.add(j)
                    q.wait_ge(ops[j]["sem"][0], ops[j]["sem"][1])
            elif j in val:
                top[eng[j]] = max(top.get(eng[j], 0), val[j])
        for f, v in top.items():
            if v > seen[e].get(f, 0):
                seen[e][f] = v
                q.wait_ge(T.sem[f], v)
        ins = ops[i]["var"][e][1](q)
        if i in wanted:
            count[e] += 1
            val[i] = count[e]
            ins.then_inc(T.sem[e], 1)
    for i in seq:
        if ops[i]["sem"] not in (None, "none") and i not in waited:
            g.wait_ge(ops[i]["sem"][0], ops[i]["sem"][1])
    g.wait_ge(T.sem.sent, sent[0])
